import numpy as np, ml_dtypes
CORES = [36,164,52,180,100,228,116,244]
N = 8
import mx_ref
BF = ml_dtypes.bfloat16
def gcols(t, e):
    v = np.concatenate([t.reshape(8, 16, -1, 4), np.zeros((8, 16, 1, 4), BF)], axis=2)
    return np.ascontiguousarray(np.stack([v[g][:, e[g]] for g in range(8)])).reshape(128, -1)
def tile(rs):
    return np.stack(rs, axis=2).reshape(128, -1).astype(BF)
def pick(q, e):
    c = np.concatenate([q[0].reshape(128, -1, 4), np.zeros((128, 1, 4), np.uint8)], axis=1); s = np.concatenate([q[1], np.ones((16, 1), np.uint8)], axis=1)
    return (np.ascontiguousarray(c[:, e].reshape(128, -1)), np.ascontiguousarray(s[:, e]))
def join(*qs):
    return (np.concatenate([q[0] for q in qs], axis=1), np.concatenate([q[1] for q in qs], axis=1))
def put(q, e, v):
    c, s = q[0].reshape(128, -1, 4).copy(), q[1].copy(); c[:, e] = v[0].reshape(128, -1, 4); s[:, e] = v[1]
    return (c.reshape(128, -1), s)
def pk(c, s):
    return (np.ascontiguousarray(c), mx_ref.live(s))
def emit(q):
    return q[0], q[1]
def packed(v, rng):
    q = [mx_ref.quantize(np.ascontiguousarray(v[r])) for r in range(N)]
    return np.stack([a for a, b in q]), np.stack([mx_ref.plane(b, rng) for a, b in q])
def f(rng, *shape):
    return mx_ref.flush((rng.standard_normal(shape, dtype=np.float32) * np.exp2(rng.integers(-2, 3, shape[:-1] + (1,)))).astype(BF))
def wide(rng, *shape, cols=0):
    v = rng.standard_normal(shape, dtype=np.float32) * np.exp2(rng.integers(-12, 13, shape)).astype(np.float32)
    if cols: v *= np.repeat(np.exp2(rng.integers(-cols, cols + 1, shape[:-2] + (1, shape[-1] // 4))) * (rng.random(shape[:-2] + (1, shape[-1] // 4)) > 0.0625), 4, axis=-1).astype(np.float32)
    return mx_ref.flush(v.astype(BF))
C, A, R = 224, 96, 3
STEP = [4, 1, 2]
def places(p):
    return np.argsort(np.argsort(-(p[::16] + np.float32(0.0)), axis=1, kind="stable"), axis=1)
def neighbours(a, b):
    below = (a[:, None] < a[:, :, None]) & (b[:, None] < b[:, :, None])
    above = below.transpose(0, 2, 1)
    def best(m, k):
        return np.where(m.any(axis=2), np.argmax(np.where(m, k[:, None], -1), axis=2), np.arange(C))
    return best(below, a), best(below, b), best(above, C - a), best(above, C - b), np.sum(below, axis=2) % 2
def parts(m):
    return np.repeat(np.repeat(m, 16, axis=0), 4, axis=1)
def toggle(t, la, lb, ua, ub, m):
    low = np.maximum(gcols(t, la).astype(np.float32), gcols(t, lb).astype(np.float32))
    high = np.minimum(gcols(t, ua).astype(np.float32), gcols(t, ub).astype(np.float32))
    v = (low + high).astype(BF)
    h = (v.astype(np.float32) - t.astype(np.float32)).astype(BF)
    new, k = t.copy(), parts(m)
    new[k] = h[k]
    return new
def gput(t, e, h):
    a, b = t.reshape(8, 16, -1, 4).copy(), h.reshape(8, 16, -1, 4)
    for g in range(8): a[g][:, e[g]] = b[g]
    return a.reshape(128, -1)
def big(v):
    v = v.astype(np.float32)
    v[np.abs(v) < np.float32(2.0 ** -16)] = 0
    return v.astype(BF)
def numbers_of(rng):
    return {"x": big(f(rng, N, 128, 4 * C)), "u": np.array(f(rng, N, 128, 512)), "v": np.array(f(rng, N, 128, 512))}
def weights(rng, still=[]):
    w = np.array(f(rng, N, 128, 2048)).reshape(N, 8, 16, 4, 8, 16, 4)
    for i in still:
        w[:, :, i] = 0
        w[:, :, :, :, :, i] = 0
    c, p = packed(w.reshape(N, 128, 2048), rng)
    return {"wc": c, "ws": p}
def signs(rng):
    return np.stack([rng.permutation(8) % 2 * 2.0 - 1.0 for r in range(N)])
def digits(k, n):
    return ((k[..., None] >> np.arange(n)) & 1) * np.exp2(np.arange(n) * 1.0)
def setup_inputs(rng):
    return {**numbers_of(rng), **weights(rng)}
def setup_inputs_ties(rng):
    d = numbers_of(rng)
    e = rng.permutation(N)
    x = d["x"].reshape(N, 8, 16, C, 4)
    for r in range(N):
        k = np.zeros(C, int) if r == e[0] else rng.permutation(C) % 3
        a = x[r][:, :8, :3].copy()
        a[:, :, 2] = 0
        x[r][:, :8] = a[:, :, k]
    x[e[1]] = 0
    u = d["u"].reshape(N, 8, 16, 128, 4)
    u[:, :, 8:, ::16] = 0
    return {"x": x.reshape(N, 128, 4 * C), "u": u.reshape(N, 128, 512), "v": d["v"], **weights(rng, range(8))}
def setup_inputs_near(rng):
    d = numbers_of(rng)
    x = d["x"].astype(np.float32).reshape(N, 8, 16, C, 4)
    u = d["u"].reshape(N, 128, 128, 4)
    u[:, :, ::16] = 0
    o, c = rng.permutation(N) % 4, signs(rng)
    z = digits(np.argsort(rng.random((N, 8, C)), axis=2) // 2, 8)
    x[:, :, 0] = 0
    x[:, :, 8:] = 0
    for r in range(N):
        if o[r] < 2: x[r, :, 0, :, 0] = c[r][:, None]
        k = z[r] * 2.0 ** -23 if o[r] < 2 else z[r] * c[r][:, None, None] * 2.0 ** -30
        x[r, :, 8] = k[:, :, :4]
        x[r, :, 9] = k[:, :, 4:]
        size = 1.0 if o[r] == 0 else 2.0 ** -30
        for h in range(0, 128, 16):
            u[r, h, h, 0] = size
            u[r, h + 8:h + 10, h] = size
    return {"x": x.reshape(N, 128, 4 * C).astype(BF), "u": u.reshape(N, 128, 512), "v": d["v"], **weights(rng, [0, 8, 9, 10, 11, 12, 13, 14, 15])}
def setup_inputs_chains(rng):
    d = numbers_of(rng)
    x = d["x"].astype(np.float32).reshape(N, 8, 16, C, 4)
    u = d["u"].reshape(N, 128, 128, 4)
    h = C // 2
    o = np.argsort(rng.random((N, 8, C)), axis=2)
    for r in range(N):
        p = r ^ STEP[0]
        if r < p:
            k = rng.permutation(8)
            for g in range(8):
                a = o[r, g]
                if k[g] == 0: o[p, g] = a
                if k[g] == 1: o[p, g] = a[::-1]
                if k[g] == 2: o[p, g] = np.concatenate([a[:1], a[1:][::-1]])
                if k[g] == 3: o[p, g] = np.concatenate([a[:-1][::-1], a[-1:]])
                if k[g] == 4: o[p, g] = np.concatenate([a[h:], a[:h]])
                if k[g] == 5: o[p, g] = np.concatenate([a[:h][::-1], a[h:][::-1]])
                if k[g] == 6: o[p, g] = a.reshape(-1, 2)[:, ::-1].reshape(-1)
    z = digits(C - 1 - np.argsort(o, axis=2), 12)
    for i in range(3): x[:, :, 8 + i] = z[:, :, :, 4 * i:4 * i + 4]
    k = np.where(rng.permutation(N) < N // 2, 2.0 ** -30, 1.0).astype(np.float32).astype(BF)
    u[:, :, ::16] = 0
    for i in range(0, 128, 16): u[:, i + 8:i + 11, i] = k[:, None, None]
    return {"x": x.reshape(N, 128, 4 * C).astype(BF), "u": u.reshape(N, 128, 512), "v": d["v"], **weights(rng, [8, 9, 10])}
def setup_inputs_huge(rng):
    d = numbers_of(rng)
    mixed = rng.permutation(8) < 4
    side = np.array([1.0 - 2.0 * (bin(r).count("1") % 2) for r in range(N)])
    c = rng.permutation(C) % 2 * 2.0 - 1.0
    k = np.where(mixed[:, None], np.argsort(rng.random((8, C)), axis=1), rng.integers(0, 32, (N, 8, C)))
    z = digits(k, 12) * np.where(mixed, 2.0 ** 21, 2.0 ** 18)[:, None, None]
    p = np.ones(8)
    p[~mixed] = rng.permutation(4) % 2 * 2.0 - 1.0
    s = np.where(mixed, side[:, None], p)
    x = np.zeros((N, 8, 16, C, 4))
    x[:, :, :8] = (s[:, :, None] * np.where(mixed[:, None], c, 1.0))[:, :, None, :, None] * 2.0 ** 30
    for i in range(3): x[:, :, 8 + i] = z[:, :, :, 4 * i:4 * i + 4] * s[:, :, None, None]
    x[:, :, 11:] = 2.0 ** 20 * (0.5 + 0.5 * rng.random((N, 8, 5, C, 4))) * rng.choice([-1.0, 1.0], (N, 8, 5, C, 4))
    u = d["u"].reshape(N, 8, 16, 128, 4)
    u[:, :, :, ::16] = 0
    w = 2.0 ** 30 * (1 - 0.125 * rng.random((8, 8, 4))) * p[:, None, None]
    q = np.ones((N, 8))
    for r in range(N): q[r, ~mixed] = rng.permutation(4) % 2 * 2.0 - 1.0
    for g in range(8):
        for h in range(8):
            if mixed[h] == mixed[g]: u[:, h, :8, 16 * g] = (q[:, g][:, None, None] * w[h]).astype(np.float32).astype(BF)
        u[:, g, 8:11, 16 * g] = 2.0 ** 30
    return {"x": x.astype(np.float32).reshape(N, 128, 4 * C).astype(BF), "u": u.reshape(N, 128, 512), "v": d["v"], **weights(rng, range(11))}
def setup_inputs_spread(rng):
    d = setup_inputs(rng)
    d["x"] = big(wide(rng, N, 128, 4 * C, cols=6))
    return d
def check_inputs(d):
    b = []
    for k in ("x", "u", "v"):
        a = np.abs(d[k].astype(np.float32))
        if not (np.isfinite(a).all() and ((a == 0) | (a >= 2.0 ** -30) & (a <= 2.0 ** 30)).all()): b.append("a value of " + k)
    if ((d["wc"] & 0x7F) == 0x7F).any(): b.append("a code of wc that is no number")
    z = np.zeros((128, 4, 4), np.float32)
    z[:, 1] = 2.0 ** -30
    z[:, 2] = 2.0 ** 30
    c, s = emit(mx_ref.quantize(z.reshape(128, 16).astype(BF)))
    for r in range(N):
        p = mx_ref.live(d["ws"][r])
        if not ((p == s[0, 0]) | (p >= s[0, 1]) & (p <= s[0, 2])).all(): b.append("a scale of ws")
    return b
def reference(x, u, v, wc, ws):
    qu = [mx_ref.quantize(u[r]) for r in range(N)]
    lay = [pk(wc[r], ws[r]) for r in range(N)]
    now = [x[r] for r in range(N)]
    for t in range(R):
        a = [places(mx_ref.matmul(qu[r], mx_ref.quantize(now[r]))) for r in range(N)]
        e, own, sent = [], [], []
        for r in range(N):
            b = a[r ^ STEP[t]]
            la, lb, ua, ub, odd = neighbours(a[r], b)
            for k in range(2): now[r] = toggle(now[r], la, lb, ua, ub, odd == k)
            e.append(np.argsort(-(a[r] + b), axis=1, kind="stable")[:, :A])
            own.append(gcols(now[r], e[r]))
            sent.append(mx_ref.quantize(own[r]))
        for r in range(N):
            q = sent[r ^ STEP[t]]
            h = tile([mx_ref.matmul(pick(lay[r], np.arange(128 * i, 128 * i + 128)), q) * np.float32(0.015625) + own[r][:, i::4].astype(np.float32) for i in range(4)])
            now[r] = gput(now[r], e[r], h)
    y = np.zeros((N, 128, C), np.float32)
    oc, osc = np.zeros((N, 128, 4 * C), np.uint8), np.zeros((N, 16, C), np.uint8)
    for r in range(N):
        q = mx_ref.quantize(now[r])
        y[r] = mx_ref.matmul(mx_ref.quantize(v[r]), q)
        oc[r], osc[r] = emit(q)
    return {"y": y, "oc": oc, "osc": osc}

@@ -1,0 +1,493 @@
+from concourse.mybir import dt, AluOpType as Op, ActivationFunctionType as Act
+
+C, A, R = 224, 96, 3
+STEP = [4, 1, 2]
+M = C // 16
+MA = A // 16
+B, MB = C - A, M - MA
+NB = C // 32
+W = C + 18
+TINY = 2.0 ** -100
+
+F8, U8, BF, F32, I32, U16 = "float8_e4m3fn_x4", "uint8", "bfloat16", "float32", "int32", "uint16"
+
+
+def _sb(dtype, **cols):
+    return {k: ("sbuf", [128, n], dtype) for k, n in cols.items()}
+
+
+SCRATCH = {
+    **_sb(F8, qu=128, qp=384, qv=128, qw=512, qx=C, ql=R * A + 128, qf=R * 128),
+    **_sb(U8, su=128, sp=384, sv=128, sw=512, sx=C, sl=R * A + 128, sf=R * 128),
+    **{k: ("psum", [128, 512], F32) for k in ("pa", "ph0", "ph1", "pw0", "pw1", "pw2", "pw3")},
+    **_sb(BF, xn=4 * C, ub=512, vb=512, sendp=R * 16, landp=R * 16),
+    **_sb(U16, sendl=R * 32, landl=R * 32), **_sb(F32, racc=8 * R, landr=8 * R),
+    **_sb(I32, ci=64, pi=4), **_sb(U16, cu=64), **_sb(F32, col=16, cc=8, tmpc=16, cfr=16, j1=16, kj=16),
+    **_sb(BF, one=C, r16=C, dg=4 * B, dgt=C, tri=NB * C, rs=4 * C, rs16=C, stl=C, stu=C, stv=C, za=2 * C + 2),
+    **_sb(F32, ta=C, af=16, ca=4),
+    **_sb(BF, df=M * C, mk=M * C, cn=M * C, bca=C, arow=C, bcb=C, brow=C, crow=C, alpha=C, erow=C, d1=C, d2=C, d3=C, d5=C),
+    **_sb(U16, c4u=4 * M, ru=16),
+    **_sb(BF, wu=C + 2, zb=2 * C + 2, ee=C, nu=C, cd=C, oa=M * W, ob=M * W, lk=2 * C, ld=2 * C, lr=4 * C, lp=4 * C, le=4 * C),
+    "nm": ("sbuf", [128, M, W], BF),
+    **_sb(F32, me=64, wj=16, nb=16, acc=16, s2=16, s3=16, pre=16, dd=64, dc=64, do=64, ds=64, l8=8 * M),
+    **_sb(I32, pt=16, odd=16, li=8 * M, lj=8 * M), **_sb(U16, lu=8 * M, lb=2 * M, lf=5 * M),
+    **_sb(F32, ka=16, kk=16, ks=C, key=C, kc=16, kb=16), **_sb(BF, junk=NB * C),
+    **_sb(BF, xa=4 * C, x1=4 * C, x2=4 * B, bd=8 * C, be=12 * C, lo=4 * C, hi=4 * C, vv=4 * C, ft=512, f64=4 * A, z64=4 * C),
+    **_sb(F32, ys=C),
+}
+SEMAPHORES = ["ev", "es", "et", "eg", "lx", "lu", "lw", "lv", "sent", "st",
+              "ap0", "ap1", "ap2", "al0", "al1", "al2", "ar0", "ar1", "ar2", "af0", "af1", "af2"]
+
+
+def rank_program(g, core, T, topo):
+    rank = T.rank_of(core)
+    if rank is None:
+        return
+    Q = {"v": g.vector, "s": g.scalar, "t": g.tensor, "g": g, "y": g.sync}
+    names = {"v": "ev", "s": "es", "t": "et", "g": "eg"}
+    count = {"v": 0, "s": 0, "t": 0, "g": 0}
+    seen = {}
+    wrote = {}
+    read = {}
+
+    def need(q, events):
+        top = {}
+        for name, n in events:
+            top[name] = max(top.get(name, 0), n)
+        for name, n in top.items():
+            if seen.get((q, name), 0) < n:
+                Q[q].wait_ge(T.sem[name], n)
+                seen[(q, name)] = n
+
+    def order(q, rd, wr):
+        ev = []
+        for k in rd:
+            ev += wrote.get(k, [])
+        for k in wr:
+            ev += wrote.get(k, []) + read.get(k, [])
+        need(q, ev)
+
+    def op(q, rd, wr, call):
+        rd, wr = rd.split(), wr.split()
+        order(q, rd, wr)
+        count[q] += 1
+        call().then_inc(T.sem[names[q]], 1)
+        e = (names[q], count[q])
+        for k in rd:
+            read.setdefault(k, []).append(e)
+        for k in wr:
+            wrote[k] = [e]
+            read[k] = []
+
+    def keys(name, ks):
+        return " ".join("%s%d" % (name, k) for k in ks)
+
+    def ts(rd, wr, out, in0, s1, s2, o0, o1=None):
+        if o1 is None:
+            op("v", rd, wr, lambda: g.vector.tensor_scalar(out, in0, s1, None, o0))
+        else:
+            op("v", rd, wr, lambda: g.vector.tensor_scalar(out, in0, s1, s2, o0, o1))
+
+    def tt(rd, wr, out, a, b, o):
+        op("v", rd, wr, lambda: g.vector.tensor_tensor(out, a, b, o))
+
+    def cp(rd, wr, out, a):
+        op("v", rd, wr, lambda: g.vector.tensor_copy(out, a))
+
+    def ms(wr, out, c):
+        op("v", "", wr, lambda: g.vector.memset(out, c))
+
+    def scan(rd, wr, out, a, b, init, o0, o1):
+        op("v", rd, wr, lambda: g.vector.tensor_tensor_scan(out, a, b, init, o0, o1))
+
+    def turn(rd, wr, out, a):
+        op("v", rd, wr, lambda: g.vector.transpose(out, a))
+
+    def act(rd, wr, out, a, f=Act.Copy, **kw):
+        op("s", rd, wr, lambda: g.scalar.activation(out, a, f, **kw))
+
+    def fill(wr, out, n, c):
+        act("one", wr, out, T.one[:, 0:n], Act.Identity, bias=c, scale=0.0)
+
+    def iota(wr, out, pat, base, cm, small=False):
+        if small:
+            op("g", "", wr, lambda: g.iota(out, pat, base, cm, allow_small_or_imprecise_dtypes=True))
+        else:
+            op("g", "", wr, lambda: g.iota(out, pat, base, cm))
+
+    def quant(rd, wr, q, s, a):
+        op("v", rd, wr, lambda: g.vector.quantize_mx(q, s, a))
+
+    def mm(rd, wr, out, lq, ls, rq, rs):
+        op("t", rd, wr, lambda: g.tensor.matmul_mx(out, lq, ls, rq, rs, True, True))
+
+    def diag(rd, wr, out, row, n):
+        scan(rd + " dg", wr, out, T.dg[:, 0:n], row, 0.0, Op.mult, Op.max)
+
+    def pl(buf, t, n=1, w=C):
+        return buf[:, t * w:(t + n) * w]
+
+    g.scalar.dma_start(T.ub[:], T.u[:]).then_inc(T.sem.lu, 16)
+    g.sync.dma_start(T.xn[:], T.x[:]).then_inc(T.sem.lx, 16)
+    g.sync.dma_start(T.qw[:].bitcast(dt.uint8), T.wc[:]).then_inc(T.sem.lw, 16)
+    g.sync.dma_start(T.sw[:], T.ws[:]).then_inc(T.sem.lw, 16)
+    g.sync.dma_start(T.vb[:], T.v[:]).then_inc(T.sem.lv, 16)
+    XN = keys("xn", range(4))
+    for k in XN.split():
+        wrote[k] = [("lx", 16)]
+    wrote["ub"], wrote["w"], wrote["vb"] = [("lu", 16)], [("lw", 32)], [("lv", 16)]
+
+    iota("pi0", T.pi[:, 0:1], [[0, 1]], 0, 1)
+    iota("cc", T.cc[:], [[32, 8]], 1, 0, True)
+    iota("one", T.one[:], [[1, C]], 1, 0, True)
+    iota("ci0", T.ci[:, 0:8], [[16, 8]], 0, 0)
+    iota("ci1", T.ci[:, 8:24], [[16, 2], [32, 4], [0, 2]], 0, 0)
+    iota("r16", T.r16[:], [[0, M], [1, 16]], 0, 0, True)
+    iota("ci2", T.ci[:, 24:38], [[1, NB], [NB, 2]], 0, 0)
+    iota("ci3", T.ci[:, 38:52], [[1, M]], 0, 0)
+    iota("j1", T.j1[:], [[16, 16]], 1, 0, True)
+    iota("tmpc", T.tmpc[:, 0:4], [[2, 4]], 0, 0, True)
+    P32, Q16 = T.col[:, 0:1], T.col[:, 1:2]
+    K1, K4, KN, KL, KQ, KS = [T.col[:, k:k + 1] for k in range(3, 9)]
+    ms("ft", T.ft[:, 4 * A:512], 0.0)
+    ms("oddz", T.odd[:], 0)
+    ts("pi0", "pi1", T.pi[:, 1:2], T.pi[:, 0:1], 31, None, Op.bitwise_and)
+    ts("pi0", "pi2", T.pi[:, 2:3], T.pi[:, 0:1], 15, None, Op.bitwise_and)
+    cp("pi1 pi2", "colq", T.col[:, 0:2], T.pi[:, 1:3])
+    ts("cc colq", "cc", T.cc[:], T.cc[:], P32, None, Op.add)
+    ts("colq", "col2", T.col[:, 2:3], Q16, 15.0, -16.0, Op.is_equal, Op.mult)
+    ts("colq", "k1", K1, Q16, 15.0, 255.0, Op.is_equal, Op.mult)
+    for k in range(4):
+        act("one", "rs%d" % k, pl(T.rs, k), T.one[:], Act.Sign, bias=-1.0)
+
+    def tri(b):
+        ts("one cc", "tri%d" % b, pl(T.tri, b), T.one[:], T.cc[:, b:b + 1], TINY, Op.is_le, Op.mult)
+
+    tri(0)
+    cp("ci0 ci1", "cu0", T.cu[:, 0:24], T.ci[:, 0:24])
+    ts("col2 colq", "col2", T.col[:, 2:3], T.col[:, 2:3], Q16, 1.0, Op.add, Op.add)
+    ts("k1", "k1", K1, K1, 1.0, 1.0 / 256, Op.add, Op.mult)
+    for b in range(1, 5):
+        tri(b)
+    quant("ub", "qu", T.qu[:], T.su[:], T.ub[:])
+    quant(XN, "qx", T.qx[:], T.sx[:], T.xn[:])
+    op("v", "qu cu0", "qp", lambda: g.vector.tensor_copy(T.qp[:].bitcast(dt.uint32), T.qu[:].bitcast(dt.uint32).indirect(T.cu[:, 0:24])))
+    act("qu cu0", "sp", T.sp[:], T.su[:].indirect(T.cu[:, 0:24]))
+
+    def consts_rows():
+        ts("r16 colq", "dg", T.dg[:, 0:C], T.r16[:], Q16, None, Op.not_equal)
+        ts("r16 col2", "dgt", T.dgt[:], T.r16[:], T.col[:, 2:3], 255.0, Op.is_equal, Op.mult)
+        cp("ci2 ci3", "cu1", T.cu[:, 24:52], T.ci[:, 24:52])
+        tt("dg dgt", "dg", T.dg[:, 0:C], T.dg[:, 0:C], T.dgt[:], Op.add)
+
+    def consts_scalar():
+        act("cc", "cfr0", T.cfr[:, 0:NB], T.cc[:, 0:NB], scale=-1.0 / 256)
+        act("cc", "cfr1", T.cfr[:, NB:M], T.cc[:, 0:NB], scale=-1.0 / 256)
+        act("k1", "k4", K4, K1, scale=4.0)
+        act("colq", "ks0", KS, Q16, scale=1.0 / 512)
+        act("k1", "kn", KN, K1, scale=-512.0)
+        act("colq", "kl", KL, Q16, Act.Identity, bias=15.0 / 512, scale=-1.0 / 512)
+        act("colq", "kq", KQ, Q16, Act.Identity, bias=260.0, scale=2.0)
+        act("j1 ks0", "j1", T.j1[:], T.j1[:], Act.Identity, bias=KS, scale=1.0 / 512)
+        act("colq", "tq", T.tmpc[:, 12:13], Q16, Act.Identity, bias=1.0)
+        act("colq", "tn", T.tmpc[:, 13:14], Q16, Act.Identity, bias=1.0, scale=-1.0)
+        act("j1", "kj", T.kj[:], T.j1[:], Act.Identity, bias=1.0, scale=-2.0)
+        fill("wuz", T.wu[:, C:C + 2], 2, 0.0)
+        fill("accz", T.acc[:], 16, 0.0)
+        act("r16 tq", "stv", T.stv[:], T.r16[:], Act.Relu, bias=T.tmpc[:, 12:13], scale=-1.0)
+        act("r16 tn", "stl", T.stl[:], T.r16[:], Act.Relu, bias=T.tmpc[:, 13:14])
+        act("stv", "stu", T.stu[:], T.stv[:], scale=-1.0)
+        act("r16", "rs16", T.rs16[:], T.r16[:], Act.Sign)
+        fill("za0", T.za[:, 0:C], C, -1.0 / 512)
+        fill("za1", T.za[:, C:C + 1], 1, C / 512.0)
+        fill("za2", T.za[:, C + 3:2 * C + 2], C - 1, 1.0 / 512)
+        for z, n in ((T.za, "za"), (T.zb, "zc")):
+            fill(n + "3", z[:, C + 1:C + 2], 1, 1.0)
+            fill(n + "4", z[:, C + 2:C + 3], 1, 4.0)
+        fill("zc5", T.zb[:, 0:1], 1, 0.0)
+        for m in range(M):
+            act("one", "nmz%d" % m, T.nm[:, m, C - 16 * m:C + 2 - 16 * m], T.one[:, 3:5])
+
+    def consts_late():
+        fill("ddz", T.dd[:, 4 * M:64], 64 - 4 * M, 0.0)
+        act("j1", "me0", T.me[:, 0:M], T.j1[:, 0:M])
+        act("j1", "me1", T.me[:, M:2 * M], T.j1[:, 0:M])
+        act("dg", "dgb", T.dg[:, C:2 * C], T.dg[:, 0:C])
+        act("dg", "dgc", T.dg[:, 2 * C:4 * B], T.dg[:, 0:4 * B - 2 * C])
+
+    def consts_lists():
+        ts("tmpc colq", "tmpc", T.tmpc[:, 0:4], T.tmpc[:, 0:4], Q16, None, Op.add)
+        ts("tmpc", "tmpd", T.tmpc[:, 4:8], T.tmpc[:, 0:4], float(M), -float(M), Op.is_ge, Op.mult)
+        tt("tmpc tmpd", "tmpe", T.tmpc[:, 8:12], T.tmpc[:, 0:4], T.tmpc[:, 4:8], Op.add)
+        cp("tmpe", "cu2", T.cu[:, 52:56], T.tmpc[:, 8:12])
+
+    SPREAD, SPREAD16, REP = T.cu[:, 24:38], T.cu[:, 38:52], T.cu[:, 52:56]
+    writes = [0]
+
+    def send(peer, out, src, sem):
+        rid, pid = topo.addr(peer, core)
+        g.remote_dma(out, src, sem, T.sem.sent, pid, rid, topo.mask(core, peer))
+        writes[0] += len(topo.engines(core, peer))
+
+    for r in range(R):
+        peer = T.cores[rank ^ STEP[r]]
+        mine = NB if rank & STEP[r] else 0
+        ne = len(topo.engines(peer, core))
+        for k, (ps, n) in enumerate(((T.pa, "pa"), (T.ph0, "ph0"), (T.ph1, "ph1"))):
+            mm("qp sp qx", n, ps[:, 0:C], pl(T.qp, k, 1, 128), pl(T.sp, k, 1, 128), T.qx[:], T.sx[:])
+        if r == 0:
+            tri(5), tri(6)
+        turn("pa", "ta0", T.ta[:, 0:64], T.pa[:, 0:64])
+        turn("pa", "ta1", T.ta[:, 64:C], T.pa[:, 64:C])
+        if r == 0:
+            consts_rows()
+        for h in range(2):
+            for b in range(NB):
+                k = h * NB + b
+                act("ph%d ta%d" % (h, b > 1), "df%d" % k, pl(T.df, k), (T.ph0, T.ph1)[h][:, 0:C], Act.Identity,
+                    bias=T.ta[:, 32 * b + 16 * h:32 * b + 16 * h + 1], scale=-1.0)
+
+        def compare(h, b0, b1):
+            k, ks = h * NB + b0, range(h * NB + b0, h * NB + b1)
+            tt(keys("df", ks) + " " + keys("tri", range(b0, b1)), keys("mk", ks), pl(T.mk, k, b1 - b0), pl(T.df, k, b1 - b0),
+               pl(T.tri, b0, b1 - b0), Op.is_lt)
+
+        def total(h, b0, b1):
+            k, ks = h * NB + b0, range(h * NB + b0, h * NB + b1)
+            scan(keys("rs", range(4)) + " " + keys("mk", ks), keys("cn", ks), pl(T.cn, k, b1 - b0), pl(T.rs, 0, b1 - b0),
+                 pl(T.mk, k, b1 - b0), 0.0, Op.mult, Op.add)
+
+        sp_, lp_ = T.sendp[:, 16 * r:16 * r + M], T.landp[:, 16 * r:16 * r + M]
+        COL, AU = T.sendl[:, 32 * r:32 * r + M], T.sendl[:, 32 * r + M:32 * r + 2 * M]
+        COLB, BU = T.landl[:, 32 * r:32 * r + M], T.landl[:, 32 * r + M:32 * r + 2 * M]
+        compare(0, 0, 1), compare(0, 1, 3), compare(0, 3, 5), compare(0, 5, 7)
+        for k in range(3):
+            act("mk%d" % k, "junk%d ca%d" % (k, k), pl(T.junk, k), pl(T.mk, k), Act.Identity, accum_out=T.ca[:, k:k + 1])
+        act("ca0 ca1 ca2", "sendp0", T.sendp[:, 16 * r:16 * r + 3], T.ca[:, 0:3])
+        total(0, 3, 7)
+        compare(1, 0, 3), compare(1, 3, 7)
+        total(1, 0, 3), total(1, 3, 7)
+        cp(keys("cn", range(3, M)), "sendp1", T.sendp[:, 16 * r + 3:16 * r + M], T.cn[:, 4 * C - 1:M * C:C])
+        order("g", ["sendp0", "sendp1"], [])
+        send(peer, lp_, sp_, T.sem["ap%d" % r])
+        wrote["landp"] = [("ap%d" % r, ne)]
+        if r == 0:
+            consts_scalar()
+        cp("sendp0 sendp1 cu1", "bca", T.bca[:], sp_.indirect(SPREAD))
+        tt("sendp0 sendp1 cfr0 cfr1", "ka", T.ka[:, 0:M], sp_, T.cfr[:, 0:M], Op.add)
+        turn("bca", "arow", T.arow[:], T.bca[:])
+        diag("arow", "d1", T.d1[:], T.arow[:], C)
+        ts("d1 k1", "au", AU, T.d1[:, 15:C:16], K1, -1.0, Op.mult, Op.add)
+        cp("one au", "crow", T.crow[:].indirect(AU), T.one[:])
+        act("d1 k1", "af", T.af[:, 0:M], T.d1[:, 15:C:16], scale=K1)
+        diag("crow", "d2", T.d2[:], T.crow[:], C)
+        ts("d2 k1", "colu", COL, T.d2[:, 15:C:16], K1, -1.0, Op.mult, Op.add)
+        order("g", ["au", "colu"], [])
+        send(peer, T.landl[:, 32 * r:32 * r + 2 * M], T.sendl[:, 32 * r:32 * r + 2 * M], T.sem["al%d" % r])
+        wrote["landl"] = [("al%d" % r, ne)]
+        for t in range(4):
+            ts("d2 k4", "c4u%d" % t, pl(T.c4u, t, 1, M), T.d2[:, 15:C:16], K4, t - 4.0, Op.mult, Op.add)
+            act(XN + " c4u%d" % t, "xa%d" % t, pl(T.xa, t), T.xn[:].indirect(pl(T.c4u, t, 1, M)))
+        tt("af kj", "kc", T.kc[:, 0:M], T.af[:, 0:M], T.kj[:, 0:M], Op.add)
+        if r == 0:
+            quant(XN, "qlz", T.ql[:, R * A:R * A + 128], T.sl[:, R * A:R * A + 128], T.xn[:, 0:512])
+            consts_lists()
+        cp("landp cu1", "bcb", T.bcb[:], lp_.indirect(SPREAD))
+        tt("landp ka", "kk", T.kk[:, 0:M], lp_, T.ka[:, 0:M], Op.add)
+        act("kk cu1", "ks", T.ks[:], T.kk[:, 0:M].indirect(SPREAD))
+        turn("bcb", "brow", T.brow[:], T.bcb[:])
+        ts("brow colu", "wu", T.wu[:, 0:C], T.brow[:].indirect(COL), 1.0 / 512, None, Op.mult)
+        diag("wu", "d3", T.d3[:], T.wu[:, 0:C], C)
+        WJ = T.wj[:, 0:M]
+        tt("wu wuz", "zb0", T.zb[:, 1:C + 1], T.wu[:, 0:C], T.wu[:, 1:C + 1], Op.subtract)
+        act("d3 k1", "wj", WJ, T.d3[:, 15:C:16], scale=K1)
+        act("d3 kn", "nb", T.nb[:, 0:M], T.d3[:, 15:C:16], scale=KN)
+
+        def masks(m):
+            if m < M - 1:
+                act("wu wj accz", "nmu%d acc%d" % (m, m), T.nm[:, m, 16:C - 16 * m], T.wu[:, 16 * m + 16:C], Act.Sign,
+                    bias=T.wj[:, m:m + 1], scale=-1.0, accum_out=T.acc[:, m:m + 1])
+            if m > 0:
+                act("wu nb", "nml%d" % m, T.nm[:, m, C + 2 - 16 * m:C + 2], T.wu[:, 0:16 * m], Act.Relu,
+                    bias=T.nb[:, m:m + 1], scale=512.0)
+
+        masks(0), masks(1)
+        tt("wj wu cu1", "ee", T.ee[:], WJ.indirect(SPREAD16), T.wu[:, 0:C], Op.subtract)
+        turn("ks", "key", T.key[:], T.ks[:])
+        act("zb0", "zb1", T.zb[:, C + 3:2 * C + 2], T.zb[:, 1:C], scale=-1.0)
+        tt("ee stu", "nu", T.nu[:], T.ee[:], T.stu[:], Op.is_lt)
+        tt("ee stl", "ndl", T.nm[:, :, C + 2:W], T.ee[:], T.stl[:], Op.is_le)
+        masks(2)
+        act("nu", "ndu", T.nm[:, :, 0:16], T.nu[:], scale=-1.0)
+        for m in range(3, M):
+            masks(m)
+
+        def scan_a(m):
+            scan("nmu%d nml%d nmz%d ndl ndu " % (m, m, m) + keys("za", range(5)), "oa%d" % m, pl(T.oa, m, 1, W),
+                 T.za[:, 16 * m:16 * m + W], T.nm[:, m, :], 4.0, Op.add, Op.min)
+
+        def scan_b(m):
+            scan("nmu%d nml%d nmz%d ndl ndu zb0 zb1 zc3 zc4 zc5" % (m, m, m), "ob%d" % m, pl(T.ob, m, 1, W),
+                 T.zb[:, 16 * m:16 * m + W], T.nm[:, m, :], 4.0, Op.add, Op.min)
+
+        scan("nu rs16", "cd", T.cd[:], T.rs16[:], T.nu[:], 0.0, Op.mult, Op.add)
+        tt("wu wj", "pre", T.pre[:, 0:M], T.wu[:, 15:C:16], WJ, Op.subtract)
+        tt("cd nb", "s2", T.s2[:, 0:M], T.cd[:, 15:C:16], T.nb[:, 0:M], Op.subtract)
+        for m in range(0, 4):
+            scan_b(m), scan_a(m)
+        cp("landl", "kb", T.kb[:, 0:M], BU)
+        scan_b(4), scan_a(4)
+        tt("kb kc", "kb", T.kb[:, 0:M], T.kb[:, 0:M], T.kc[:, 0:M], Op.add)
+        act("s2 kq", "s3", T.s3[:, 0:M], T.s2[:, 0:M], Act.Identity, bias=KQ, scale=2.0)
+        act("wj", "me2", T.me[:, 2 * M:3 * M], WJ)
+        act("wj", "me3", T.me[:, 3 * M:4 * M], WJ)
+        if r == 0:
+            consts_late()
+        for m in range(NB):
+            act("key kb", "junk%d racc%d" % (m, m), pl(T.junk, m), T.key[:], Act.Sign, bias=T.kb[:, mine + m:mine + m + 1], scale=-1.0,
+                accum_out=T.racc[:, 8 * r + m:8 * r + m + 1])
+        order("g", keys("racc", range(NB)).split(), [])
+        send(peer, T.landr[:, 8 * r:8 * r + NB], T.racc[:, 8 * r:8 * r + NB], T.sem["ar%d" % r])
+        wrote["landr"] = [("ar%d" % r, ne)]
+        act("arow landl", "alpha", T.alpha[:], T.arow[:].indirect(COLB))
+        for m in range(5, M - 1):
+            scan_b(m), scan_a(m)
+        scan_b(M - 1)
+        tt("s3 accz " + keys("acc", range(M - 1)), "pt", T.pt[:, 0:M], T.s3[:, 0:M], T.acc[:, 0:M], Op.subtract)
+        scan_a(M - 1)
+        OA, OB = keys("oa", range(M)), keys("ob", range(M))
+        up = slice(C + 1, (M - 1) * (W - 16) + C + 2, W - 16)
+        dn = slice(W - 1, M * W, W)
+        tt(OB + " pre", "dd2", T.dd[:, 2 * M:3 * M], T.pre[:, 0:M], T.ob[:, dn], Op.subtract)
+        tt(OB + " wj", "dd3", T.dd[:, 3 * M:4 * M], T.ob[:, up], WJ, Op.subtract)
+        ts(OA + " kl", "dd0", T.dd[:, 0:M], T.oa[:, dn], -1.0, KL, Op.mult, Op.add)
+        tt(OA + " j1", "dd1", T.dd[:, M:2 * M], T.oa[:, up], T.j1[:, 0:M], Op.subtract)
+        ts("pt oddz", "odd", T.odd[:, 0:M], T.pt[:, 0:M], 1, 1, Op.arith_shift_right, Op.bitwise_and)
+        ts("dd0 dd1 dd2 dd3 ddz", "dc", T.dc[:], T.dd[:], -0.5, 0.5, Op.max, Op.min)
+        ME = "me0 me1 me2 me3"
+        tt("odd dc cu2", "do", T.do[:], T.odd[:].indirect(REP), T.dc[:], Op.mult)
+        tt("dc " + ME, "ds", T.ds[:, 0:4 * M], T.dc[:, 0:4 * M], T.me[:, 0:4 * M], Op.add)
+        tt("do " + ME, "l81", T.l8[:, 4 * M:8 * M], T.do[:, 0:4 * M], T.me[:, 0:4 * M], Op.add)
+        tt("do ds", "l80", T.l8[:, 0:4 * M], T.ds[:, 0:4 * M], T.do[:, 0:4 * M], Op.subtract)
+        ts("l80 l81", "li", T.li[:], T.l8[:], 512.0, 255.0, Op.mult, Op.add)
+        ts("li", "lj", T.lj[:], T.li[:], 255, None, Op.bitwise_and)
+        cp("lj", "lu", T.lu[:], T.lj[:])
+        act("alpha lu", "lk1", pl(T.lk, 1), T.alpha[:].indirect(T.lu[:, 3 * M:4 * M]))
+        cp("alpha lu", "lk0", pl(T.lk, 0), T.alpha[:].indirect(T.lu[:, 2 * M:3 * M]))
+        act("one lu", "lr0", pl(T.lr, 0, 2), T.one[:].indirect(T.lu[:, 4 * M:6 * M]))
+        diag("lk0 lk1 dgb", "ld", T.ld[:], T.lk[:], 2 * C)
+        ts("ld k1", "lb", T.lb[:], T.ld[:, 15:2 * C:16], K1, -1.0, Op.mult, Op.add)
+
+        def far(t):
+            act("xa%d lb" % t, "bd%d" % t, pl(T.bd, 2 * t, 2), pl(T.xa, t).indirect(T.lb[:]))
+
+        def low(t):
+            tt("xa%d lu bd%d" % (t, t), "lo%d" % t, pl(T.lo, t), pl(T.xa, t).indirect(T.lu[:, 0:M]), pl(T.bd, 2 * t), Op.max)
+
+        def high(t):
+            tt("xa%d lu bd%d" % (t, t), "hi%d" % t, pl(T.hi, t), pl(T.xa, t).indirect(T.lu[:, M:2 * M]), pl(T.bd, 2 * t + 1), Op.min)
+
+        def add(t, n):
+            ks = range(t, t + n)
+            tt(keys("lo", ks) + " " + keys("hi", ks), keys("vv", ks), pl(T.vv, t, n), pl(T.lo, t, n), pl(T.hi, t, n), Op.add)
+
+        def sub(t, n):
+            ks = range(t, t + n)
+            tt(keys("vv", ks) + " " + keys("xa", ks), keys("x1", ks), pl(T.x1, t, n), pl(T.vv, t, n), pl(T.xa, t, n), Op.subtract)
+
+        part = ((0, A, 0, MA), (4 * A, B, 5 * MA, MB))
+        own = (T.lf[:, 4 * MA:5 * MA], T.lf[:, 5 * MA + 4 * MB:5 * M])
+
+        def relist(i):
+            o, w = part[i][0:2]
+            for k in range(4):
+                act("lr0 lr1 own%d" % i, "lp%d%d" % (i, k), T.lp[:, o + k * w:o + (k + 1) * w], pl(T.lr, k).indirect(own[i]))
+
+        def lists(i):
+            o, w, c, n = part[i]
+            diag(keys("lp%d" % i, range(4)) + " dgb dgc", "le%d" % i, T.le[:, o:o + 4 * w], T.lp[:, o:o + 4 * w], 4 * w)
+            ts("le%d k1" % i, "lf%d" % i, T.lf[:, c:c + 4 * n], T.le[:, o + 15:o + 4 * w:16], K1, -1.0, Op.mult, Op.add)
+
+        far(0), far(1), far(2)
+        cp("alpha lu", "lr1", pl(T.lr, 2, 2), T.alpha[:].indirect(T.lu[:, 6 * M:8 * M]))
+        ts(keys("racc", range(NB)), "ru0", T.ru[:, mine:mine + NB], T.racc[:, 8 * r:8 * r + NB], -0.5, (C - 1) / 2.0, Op.mult, Op.add)
+        low(0), high(0)
+        ts("landr", "ru1", T.ru[:, NB - mine:M - mine], T.landr[:, 8 * r:8 * r + NB], -0.5, (C - 1) / 2.0, Op.mult, Op.add)
+        low(1)
+        cp("arow ru0 ru1", "erow", T.erow[:].indirect(T.ru[:, 0:M]), T.arow[:])
+        far(3)
+        high(1)
+        diag("erow", "d5", T.d5[:], T.erow[:], C)
+        add(0, 2)
+        ts("d5 k1", "own0", own[0], T.d5[:, 15:A:16], K1, -1.0, Op.mult, Op.add)
+        relist(0)
+        ts("d5 k1", "own1", own[1], T.d5[:, A + 15:C:16], K1, -1.0, Op.mult, Op.add)
+        sub(0, 2), low(2), high(2)
+
+        def far2(i, t):
+            o, w, c, n = part[i]
+            act("x1%d lf%d own%d" % (t, i, i), "be%d%d" % (i, t), T.be[:, 3 * (o + t * w):3 * (o + t * w + w)],
+                pl(T.x1, t).indirect(T.lf[:, c + 2 * n:c + 5 * n]))
+
+        def near2(i, t, k):
+            o, w, c, n = part[i]
+            buf, name = ((T.lo, "lo"), (T.hi, "hi"))[k]
+            tt("x1%d lf%d be%d%d" % (t, i, i, t), "%s%d" % (name, t + 4), pl(buf, t, 1, w), pl(T.x1, t).indirect(T.lf[:, c + k * n:c + (k + 1) * n]),
+               T.be[:, 3 * (o + t * w) + k * w:3 * (o + t * w) + (k + 1) * w], (Op.max, Op.min)[k])
+
+        def add2(i, t):
+            w = part[i][1]
+            tt("lo%d lo%d hi%d hi%d" % (t + 4, t + 5, t + 4, t + 5), "vv%d vv%d" % (t + 4, t + 5), pl(T.vv, t, 2, w), pl(T.lo, t, 2, w), pl(T.hi, t, 2, w), Op.add)
+
+        def sub2(i, t):
+            o, w, c, n = part[i]
+            out, name = ((T.ft[:, t:4 * A:4], "ft"), (pl(T.x2, t, 1, B), "x2"))[i]
+            tt("vv%d be%d%d" % (t + 4, i, t), "%s%d" % (name, t), out, pl(T.vv, t, 1, w),
+               T.be[:, 3 * (o + t * w) + 2 * w:3 * (o + t * w + w)], Op.subtract)
+            if i:
+                act("x2%d" % t, "zx%d" % t, T.z64[:, t * C + A:(t + 1) * C], pl(T.x2, t, 1, B), scale=64.0)
+
+        lists(0)
+        far2(0, 0), far2(0, 1)
+        low(3), high(3), add(2, 2), near2(0, 0, 0), sub(2, 2)
+        far2(0, 2), far2(0, 3)
+        relist(1)
+        near2(0, 0, 1), near2(0, 1, 0), near2(0, 1, 1), near2(0, 2, 0), add2(0, 0), near2(0, 2, 1), sub2(0, 0)
+        near2(0, 3, 0), near2(0, 3, 1), sub2(0, 1), add2(0, 2), sub2(0, 2), sub2(0, 3)
+        f0, l0 = 128 * r, (R - 1 - r) * A
+        quant("ft " + keys("ft", range(4)), "qf", T.qf[:, f0:f0 + 128], T.sf[:, f0:f0 + 128], T.ft[:])
+        order("g", ["qf"], [])
+        send(peer, T.ql[:, l0:l0 + A].bitcast(dt.uint8), T.qf[:, f0:f0 + A].bitcast(dt.uint8), T.sem["af%d" % r])
+        send(peer, T.sl[:, l0:l0 + A], T.sf[:, f0:f0 + A], T.sem["af%d" % r])
+        wrote["ql"] = [("af%d" % r, 2 * ne)]
+        lists(1)
+        far2(1, 0), far2(1, 1), far2(1, 2), far2(1, 3)
+        ts(keys("ft", range(4)), "f64", T.f64[:], T.ft[:, 0:4 * A], 64.0, None, Op.mult)
+        if r == 0:
+            quant("vb", "qv", T.qv[:], T.sv[:], T.vb[:])
+        near2(1, 0, 0), near2(1, 0, 1), near2(1, 1, 0), near2(1, 1, 1), add2(1, 0), near2(1, 2, 0), sub2(1, 0)
+        near2(1, 2, 1), sub2(1, 1), near2(1, 3, 0), near2(1, 3, 1), add2(1, 2), sub2(1, 2), sub2(1, 3)
+        for b in range(4):
+            mm("w ql qlz", "pw%d" % b, T["pw%d" % b][:, 0:128], pl(T.qw, b, 1, 128), pl(T.sw, b, 1, 128),
+               T.ql[:, l0:l0 + 128], T.sl[:, l0:l0 + 128])
+        for b in range(4):
+            tt("pw%d f64" % b, "zh%d" % b, T.z64[:, b * C:b * C + A], T["pw%d" % b][:, 0:A], T.f64[:, b:4 * A:4], Op.add)
+        for t in range(4):
+            src = pl(T.z64, t).indirect(T.ru[:, 0:M])
+            if t < 2:
+                act("zx%d zh%d ru0 ru1" % (t, t), "xn%d" % t, T.xn[:, t:4 * C:4], src, scale=0.015625)
+            else:
+                ts("zx%d zh%d ru0 ru1" % (t, t), "xn%d" % t, T.xn[:, t:4 * C:4], src, 0.015625, None, Op.mult)
+        quant(XN, "qx", T.qx[:], T.sx[:], T.xn[:])
+
+    mm("qv qx", "pa", T.pa[:, 0:C], T.qv[:], T.sv[:], T.qx[:], T.sx[:])
+    order("y", ["qx"], [])
+    g.sync.dma_start(T.oc[:], T.qx[:].bitcast(dt.uint8)).then_inc(T.sem.st, 16)
+    order("s", ["qx"], [])
+    for k in range(4):
+        (g.scalar, g.sync)[k % 2].dma_start(T.osc[4 * k:4 * k + 4, :], T.sx[32 * k:32 * k + 4, :]).then_inc(T.sem.st, 16)
+    cp("pa", "ys", T.ys[:], T.pa[:, 0:C])
+    order("s", ["ys"], [])
+    g.scalar.dma_start(T.y[:], T.ys[:]).then_inc(T.sem.st, 16)
+    need("g", [("ev", count["v"]), ("es", count["s"]), ("et", count["t"]), ("eg", count["g"]),
+               ("sent", writes[0]), ("st", 96)])

@@ -20,23 +20,24 @@ SCRATCH = {
     **_sb(F8, qu=128, qp=384, qv=128, qw=512, qx=C, ql=R * A + 128, qf=R * 128),
     **_sb(U8, su=128, sp=384, sv=128, sw=512, sx=C, sl=R * A + 128, sf=R * 128),
     **{k: ("psum", [128, 512], F32) for k in ("pa", "ph0", "ph1", "pw0", "pw1", "pw2", "pw3")},
-    **_sb(BF, xn=4 * C, ub=512, vb=512, sendp=R * 16, landp=R * 16),
-    **_sb(U16, sendl=R * 32, landl=R * 32), **_sb(F32, racc=8 * R, landr=8 * R),
-    **_sb(I32, ci=64, pi=4), **_sb(U16, cu=64), **_sb(F32, col=16, cc=8, tmpc=16, cfr=16, j1=16, kj=16),
+    **_sb(BF, xn=4 * C, ub=512, vb=512, sendp=R * 16, landp=R * 16, senda=R * 16, landa=R * 16),
+    **_sb(U16, sendl=R * 16, landl=R * 16), "racc": ("sbuf", [128, 2 * R, 8], F32),
+    **_sb(I32, ci=66, pi=4), **_sb(U16, cu=74), **_sb(F32, col=16, cc=8, tmpc=32, cfr=16, j1=16, kj=16),
     **_sb(BF, one=C, r16=C, dg=4 * B, dgt=C, tri=NB * C, rs=4 * C, rs16=C, stl=C, stu=C, stv=C, za=2 * C + 2),
-    **_sb(F32, ta=C, af=16, ca=4),
+    **_sb(F32, ta=C, ca=8),
     **_sb(BF, df=M * C, mk=M * C, cn=M * C, bca=C, arow=C, bcb=C, brow=C, crow=C, alpha=C, erow=C, d1=C, d2=C, d3=C, d5=C),
-    **_sb(U16, c4u=4 * M, ru=16),
-    **_sb(BF, wu=C + 2, zb=2 * C + 2, ee=C, nu=C, cd=C, oa=M * W, ob=M * W, lk=2 * C, ld=2 * C, lr=4 * C, lp=4 * C, le=4 * C),
+    **_sb(U16, au=16, c4u=4 * M, ru=16),
+    **_sb(BF, wu=C + 2, zb=2 * C + 2, ee=C, nu=C, cd=C, oo=2 * M * W, lk=2 * C, ld=2 * C, lr=4 * C, lp=4 * C, le=4 * C),
     "nm": ("sbuf", [128, M, W], BF),
-    **_sb(F32, me=64, wj=16, nb=16, acc=16, s2=16, s3=16, pre=16, dd=64, dc=64, do=64, ds=64, l8=8 * M),
-    **_sb(I32, pt=16, odd=16, li=8 * M, lj=8 * M), **_sb(U16, lu=8 * M, lb=2 * M, lf=5 * M),
+    **_sb(F32, me=8 * M, wj=16, nb=16, acc=16, acs=16, s2=16, s3=8 * M, pre=2 * M, dd=4 * M, d8=8 * M, dc=8 * M),
+    **_sb(I32, pt=8 * M, fl=8 * M, li=8 * M, lj=8 * M), **_sb(U16, lu=8 * M, lb=2 * M, lf=5 * M),
     **_sb(F32, ka=16, kk=16, ks=C, key=C, kc=16, kb=16), **_sb(BF, junk=NB * C),
-    **_sb(BF, xa=4 * C, x1=4 * C, x2=4 * B, bd=8 * C, be=12 * C, lo=4 * C, hi=4 * C, vv=4 * C, ft=512, f64=4 * A, z64=4 * C),
+    **_sb(BF, xp=4 * C, xs=4 * C, xa=4 * C, x1=4 * C, x2=4 * B, bd=8 * C, be=8 * C, lo=4 * C, hi=4 * C, vv=4 * C,
+          ft=512, f64=4 * A, z64=4 * C),
     **_sb(F32, ys=C),
 }
-SEMAPHORES = ["ev", "es", "et", "eg", "lx", "lu", "lw", "lv", "sent", "st",
-              "ap0", "ap1", "ap2", "al0", "al1", "al2", "ar0", "ar1", "ar2", "af0", "af1", "af2"]
+SEMAPHORES = ["ev", "es", "et", "eg", "lx", "lu", "lw", "lv", "sent", "st", "ap0", "ap1", "ap2", "al0", "al1", "al2",
+              "aa0", "aa1", "aa2", "ar0", "ar1", "ar2", "af0", "af1", "af2"]
 
 
 def rank_program(g, core, T, topo):
@@ -145,12 +146,19 @@ def rank_program(g, core, T, topo):
     iota("r16", T.r16[:], [[0, M], [1, 16]], 0, 0, True)
     iota("ci2", T.ci[:, 24:38], [[1, NB], [NB, 2]], 0, 0)
     iota("ci3", T.ci[:, 38:52], [[1, M]], 0, 0)
+    iota("ci4", T.ci[:, 52:66], [[C, NB], [NB * C, 2]], C - 1, 0)
     iota("j1", T.j1[:], [[16, 16]], 1, 0, True)
-    iota("tmpc", T.tmpc[:, 0:4], [[2, 4]], 0, 0, True)
+    iota("tmpc", T.tmpc[:, 0:8], [[2, 8]], 0, 0, True)
+    iota("wuz", T.wu[:, C:C + 2], [[0, 2]], 0, 0, True)
+    iota("accz", T.acc[:], [[0, 16]], 0, 0, True)
+    iota("za3 za4", T.za[:, C + 1:C + 3], [[3, 2]], 1, 0, True)
+    iota("zc3 zc4", T.zb[:, C + 1:C + 3], [[3, 2]], 1, 0, True)
+    iota("zc5", T.zb[:, 0:1], [[0, 1]], 0, 0, True)
+    for m in range(M):
+        iota("nmz%d" % m, T.nm[:, m, C - 16 * m:C + 2 - 16 * m], [[0, 2]], 4, 0, True)
     P32, Q16 = T.col[:, 0:1], T.col[:, 1:2]
     K1, K4, KN, KL, KQ, KS = [T.col[:, k:k + 1] for k in range(3, 9)]
     ms("ft", T.ft[:, 4 * A:512], 0.0)
-    ms("oddz", T.odd[:], 0)
     ts("pi0", "pi1", T.pi[:, 1:2], T.pi[:, 0:1], 31, None, Op.bitwise_and)
     ts("pi0", "pi2", T.pi[:, 2:3], T.pi[:, 0:1], 15, None, Op.bitwise_and)
     cp("pi1 pi2", "colq", T.col[:, 0:2], T.pi[:, 1:3])
@@ -177,7 +185,7 @@ def rank_program(g, core, T, topo):
     def consts_rows():
         ts("r16 colq", "dg", T.dg[:, 0:C], T.r16[:], Q16, None, Op.not_equal)
         ts("r16 col2", "dgt", T.dgt[:], T.r16[:], T.col[:, 2:3], 255.0, Op.is_equal, Op.mult)
-        cp("ci2 ci3", "cu1", T.cu[:, 24:52], T.ci[:, 24:52])
+        cp("ci2 ci3 ci4", "cu1", T.cu[:, 24:66], T.ci[:, 24:66])
         tt("dg dgt", "dg", T.dg[:, 0:C], T.dg[:, 0:C], T.dgt[:], Op.add)
 
     def consts_scalar():
@@ -187,41 +195,35 @@ def rank_program(g, core, T, topo):
         act("colq", "ks0", KS, Q16, scale=1.0 / 512)
         act("k1", "kn", KN, K1, scale=-512.0)
         act("colq", "kl", KL, Q16, Act.Identity, bias=15.0 / 512, scale=-1.0 / 512)
-        act("colq", "kq", KQ, Q16, Act.Identity, bias=260.0, scale=2.0)
+        act("colq", "kq", KQ, Q16, Act.Identity, bias=260.0 * 256, scale=512.0)
         act("j1 ks0", "j1", T.j1[:], T.j1[:], Act.Identity, bias=KS, scale=1.0 / 512)
-        act("colq", "tq", T.tmpc[:, 12:13], Q16, Act.Identity, bias=1.0)
-        act("colq", "tn", T.tmpc[:, 13:14], Q16, Act.Identity, bias=1.0, scale=-1.0)
-        act("j1", "kj", T.kj[:], T.j1[:], Act.Identity, bias=1.0, scale=-2.0)
-        fill("wuz", T.wu[:, C:C + 2], 2, 0.0)
-        fill("accz", T.acc[:], 16, 0.0)
-        act("r16 tq", "stv", T.stv[:], T.r16[:], Act.Relu, bias=T.tmpc[:, 12:13], scale=-1.0)
-        act("r16 tn", "stl", T.stl[:], T.r16[:], Act.Relu, bias=T.tmpc[:, 13:14])
+        act("colq", "tq", T.tmpc[:, 24:25], Q16, Act.Identity, bias=1.0)
+        act("colq", "tn", T.tmpc[:, 25:26], Q16, Act.Identity, bias=1.0, scale=-1.0)
+        act("j1", "kj", T.kj[:], T.j1[:], scale=-2.0)
+
+    def consts_masks():
+        act("r16 tq", "stv", T.stv[:], T.r16[:], Act.Relu, bias=T.tmpc[:, 24:25], scale=-1.0)
+        act("r16 tn", "stl", T.stl[:], T.r16[:], Act.Relu, bias=T.tmpc[:, 25:26])
         act("stv", "stu", T.stu[:], T.stv[:], scale=-1.0)
         act("r16", "rs16", T.rs16[:], T.r16[:], Act.Sign)
         fill("za0", T.za[:, 0:C], C, -1.0 / 512)
         fill("za1", T.za[:, C:C + 1], 1, C / 512.0)
         fill("za2", T.za[:, C + 3:2 * C + 2], C - 1, 1.0 / 512)
-        for z, n in ((T.za, "za"), (T.zb, "zc")):
-            fill(n + "3", z[:, C + 1:C + 2], 1, 1.0)
-            fill(n + "4", z[:, C + 2:C + 3], 1, 4.0)
-        fill("zc5", T.zb[:, 0:1], 1, 0.0)
-        for m in range(M):
-            act("one", "nmz%d" % m, T.nm[:, m, C - 16 * m:C + 2 - 16 * m], T.one[:, 3:5])
 
     def consts_late():
-        fill("ddz", T.dd[:, 4 * M:64], 64 - 4 * M, 0.0)
-        act("j1", "me0", T.me[:, 0:M], T.j1[:, 0:M])
-        act("j1", "me1", T.me[:, M:2 * M], T.j1[:, 0:M])
+        act("one kl", "pre0", T.pre[:, 0:M], T.one[:, 0:M], Act.Identity, bias=KL, scale=0.0)
+        for k in (0, 1, 4, 5):
+            act("j1", "me%d" % k, pl(T.me, k, 1, M), T.j1[:, 0:M], Act.Identity, bias=255.0, scale=512.0)
         act("dg", "dgb", T.dg[:, C:2 * C], T.dg[:, 0:C])
         act("dg", "dgc", T.dg[:, 2 * C:4 * B], T.dg[:, 0:4 * B - 2 * C])
 
     def consts_lists():
-        ts("tmpc colq", "tmpc", T.tmpc[:, 0:4], T.tmpc[:, 0:4], Q16, None, Op.add)
-        ts("tmpc", "tmpd", T.tmpc[:, 4:8], T.tmpc[:, 0:4], float(M), -float(M), Op.is_ge, Op.mult)
-        tt("tmpc tmpd", "tmpe", T.tmpc[:, 8:12], T.tmpc[:, 0:4], T.tmpc[:, 4:8], Op.add)
-        cp("tmpe", "cu2", T.cu[:, 52:56], T.tmpc[:, 8:12])
+        ts("tmpc colq", "tmpc", T.tmpc[:, 0:8], T.tmpc[:, 0:8], Q16, None, Op.add)
+        ts("tmpc", "tmpd", T.tmpc[:, 8:16], T.tmpc[:, 0:8], float(M), -float(M), Op.is_ge, Op.mult)
+        tt("tmpc tmpd", "tmpe", T.tmpc[:, 16:24], T.tmpc[:, 0:8], T.tmpc[:, 8:16], Op.add)
+        cp("tmpe", "cu2", T.cu[:, 66:74], T.tmpc[:, 16:24])
 
-    SPREAD, SPREAD16, REP = T.cu[:, 24:38], T.cu[:, 38:52], T.cu[:, 52:56]
+    SPREAD, SPREAD16, ENDS, REP = T.cu[:, 24:38], T.cu[:, 38:52], T.cu[:, 52:66], T.cu[:, 66:73]
     writes = [0]
 
     def send(peer, out, src, sem):
@@ -231,7 +233,8 @@ def rank_program(g, core, T, topo):
 
     for r in range(R):
         peer = T.cores[rank ^ STEP[r]]
-        mine = NB if rank & STEP[r] else 0
+        half = 1 if rank & STEP[r] else 0
+        mine = NB * half
         ne = len(topo.engines(peer, core))
         for k, (ps, n) in enumerate(((T.pa, "pa"), (T.ph0, "ph0"), (T.ph1, "ph1"))):
             mm("qp sp qx", n, ps[:, 0:C], pl(T.qp, k, 1, 128), pl(T.sp, k, 1, 128), T.qx[:], T.sx[:])
@@ -241,11 +244,12 @@ def rank_program(g, core, T, topo):
         turn("pa", "ta1", T.ta[:, 64:C], T.pa[:, 64:C])
         if r == 0:
             consts_rows()
-        for h in range(2):
-            for b in range(NB):
-                k = h * NB + b
-                act("ph%d ta%d" % (h, b > 1), "df%d" % k, pl(T.df, k), (T.ph0, T.ph1)[h][:, 0:C], Act.Identity,
-                    bias=T.ta[:, 32 * b + 16 * h:32 * b + 16 * h + 1], scale=-1.0)
+        for b in (NB - 1, NB - 2):
+            ts("ta1", "ph1 df%d" % (NB + b), pl(T.df, NB + b), T.ph1[:, 0:C], -1.0, T.ta[:, 32 * b + 16:32 * b + 17], Op.mult, Op.add)
+        for k in range(M - 2):
+            h, b = k // NB, k % NB
+            act("ph%d ta%d" % (h, b > 1), "df%d" % k, pl(T.df, k), (T.ph0, T.ph1)[h][:, 0:C], Act.Identity,
+                bias=T.ta[:, 32 * b + 16 * h:32 * b + 16 * h + 1], scale=-1.0)
 
         def compare(h, b0, b1):
             k, ks = h * NB + b0, range(h * NB + b0, h * NB + b1)
@@ -258,37 +262,56 @@ def rank_program(g, core, T, topo):
                  pl(T.mk, k, b1 - b0), 0.0, Op.mult, Op.add)
 
         sp_, lp_ = T.sendp[:, 16 * r:16 * r + M], T.landp[:, 16 * r:16 * r + M]
-        COL, AU = T.sendl[:, 32 * r:32 * r + M], T.sendl[:, 32 * r + M:32 * r + 2 * M]
-        COLB, BU = T.landl[:, 32 * r:32 * r + M], T.landl[:, 32 * r + M:32 * r + 2 * M]
-        compare(0, 0, 1), compare(0, 1, 3), compare(0, 3, 5), compare(0, 5, 7)
-        for k in range(3):
-            act("mk%d" % k, "junk%d ca%d" % (k, k), pl(T.junk, k), pl(T.mk, k), Act.Identity, accum_out=T.ca[:, k:k + 1])
-        act("ca0 ca1 ca2", "sendp0", T.sendp[:, 16 * r:16 * r + 3], T.ca[:, 0:3])
-        total(0, 3, 7)
-        compare(1, 0, 3), compare(1, 3, 7)
-        total(1, 0, 3), total(1, 3, 7)
-        cp(keys("cn", range(3, M)), "sendp1", T.sendp[:, 16 * r + 3:16 * r + M], T.cn[:, 4 * C - 1:M * C:C])
-        order("g", ["sendp0", "sendp1"], [])
+        COL, COLB, AU = T.sendl[:, 16 * r:16 * r + M], T.landl[:, 16 * r:16 * r + M], T.au[:, 0:M]
+        AF, BF_ = T.senda[:, 16 * r:16 * r + M], T.landa[:, 16 * r:16 * r + M]
+        compare(0, 0, 1), compare(0, 1, 3), compare(0, 3, 5)
+        total(0, 0, 3)
+        compare(0, 5, 7), compare(1, 0, 2)
+        total(0, 3, 5)
+        compare(1, 2, 5), compare(1, 5, 7)
+        for k in range(6):
+            act("mk%d" % (5 + k), "junk%d ca%d" % (k, k), pl(T.junk, k), pl(T.mk, 5 + k), Act.Identity, accum_out=T.ca[:, k:k + 1])
+        act(keys("ca", range(6)), keys("cn", range(5, 11)), T.cn[:, 6 * C - 1:11 * C:C], T.ca[:, 0:6])
+        total(1, 4, 7)
+        act(keys("cn", range(M)), "sendp", sp_, T.cn[:, C - 1:M * C:C])
+        order("g", ["sendp"], [])
         send(peer, lp_, sp_, T.sem["ap%d" % r])
         wrote["landp"] = [("ap%d" % r, ne)]
         if r == 0:
             consts_scalar()
-        cp("sendp0 sendp1 cu1", "bca", T.bca[:], sp_.indirect(SPREAD))
-        tt("sendp0 sendp1 cfr0 cfr1", "ka", T.ka[:, 0:M], sp_, T.cfr[:, 0:M], Op.add)
+
+        def planes(ts_):
+            for t in ts_:
+                act("xn%d" % t, "xp%d" % t, pl(T.xp, t), T.xn[:, t:4 * C:4])
+
+        cp(keys("cn", range(M)) + " cu1", "bca", T.bca[:], T.cn[:].indirect(ENDS))
+        if r > 0:
+            planes((0, 1))
+        tt("sendp cfr0 cfr1", "ka", T.ka[:, 0:M], sp_, T.cfr[:, 0:M], Op.add)
         turn("bca", "arow", T.arow[:], T.bca[:])
         diag("arow", "d1", T.d1[:], T.arow[:], C)
         ts("d1 k1", "au", AU, T.d1[:, 15:C:16], K1, -1.0, Op.mult, Op.add)
         cp("one au", "crow", T.crow[:].indirect(AU), T.one[:])
-        act("d1 k1", "af", T.af[:, 0:M], T.d1[:, 15:C:16], scale=K1)
+        act("d1 k1", "af", AF, T.d1[:, 15:C:16], scale=K1)
+        if r == 0:
+            consts_masks()
+        else:
+            planes((2, 3))
+        order("g", ["af"], [])
+        send(peer, BF_, AF, T.sem["aa%d" % r])
+        wrote["landa"] = [("aa%d" % r, ne)]
+        tt("af kj", "kc", T.kc[:, 0:M], AF, T.kj[:, 0:M], Op.add)
         diag("crow", "d2", T.d2[:], T.crow[:], C)
         ts("d2 k1", "colu", COL, T.d2[:, 15:C:16], K1, -1.0, Op.mult, Op.add)
-        order("g", ["au", "colu"], [])
-        send(peer, T.landl[:, 32 * r:32 * r + 2 * M], T.sendl[:, 32 * r:32 * r + 2 * M], T.sem["al%d" % r])
+        order("g", ["colu"], [])
+        send(peer, COLB, COL, T.sem["al%d" % r])
         wrote["landl"] = [("al%d" % r, ne)]
         for t in range(4):
-            ts("d2 k4", "c4u%d" % t, pl(T.c4u, t, 1, M), T.d2[:, 15:C:16], K4, t - 4.0, Op.mult, Op.add)
-            act(XN + " c4u%d" % t, "xa%d" % t, pl(T.xa, t), T.xn[:].indirect(pl(T.c4u, t, 1, M)))
-        tt("af kj", "kc", T.kc[:, 0:M], T.af[:, 0:M], T.kj[:, 0:M], Op.add)
+            if r == 0:
+                ts("d2 k4", "c4u%d" % t, pl(T.c4u, t, 1, M), T.d2[:, 15:C:16], K4, t - 4.0, Op.mult, Op.add)
+                act(XN + " c4u%d" % t, "xa%d" % t, pl(T.xa, t), T.xn[:].indirect(pl(T.c4u, t, 1, M)))
+            else:
+                act("xp%d colu" % t, "xa%d" % t, pl(T.xa, t), pl(T.xp, t).indirect(COL))
         if r == 0:
             quant(XN, "qlz", T.ql[:, R * A:R * A + 128], T.sl[:, R * A:R * A + 128], T.xn[:, 0:512])
             consts_lists()
@@ -323,53 +346,49 @@ def rank_program(g, core, T, topo):
             masks(m)
 
         def scan_a(m):
-            scan("nmu%d nml%d nmz%d ndl ndu " % (m, m, m) + keys("za", range(5)), "oa%d" % m, pl(T.oa, m, 1, W),
+            scan("nmu%d nml%d nmz%d ndl ndu " % (m, m, m) + keys("za", range(5)), "oa%d" % m, pl(T.oo, m, 1, W),
                  T.za[:, 16 * m:16 * m + W], T.nm[:, m, :], 4.0, Op.add, Op.min)
 
         def scan_b(m):
-            scan("nmu%d nml%d nmz%d ndl ndu zb0 zb1 zc3 zc4 zc5" % (m, m, m), "ob%d" % m, pl(T.ob, m, 1, W),
+            scan("nmu%d nml%d nmz%d ndl ndu zb0 zb1 zc3 zc4 zc5" % (m, m, m), "ob%d" % m, pl(T.oo, M + m, 1, W),
                  T.zb[:, 16 * m:16 * m + W], T.nm[:, m, :], 4.0, Op.add, Op.min)
 
         scan("nu rs16", "cd", T.cd[:], T.rs16[:], T.nu[:], 0.0, Op.mult, Op.add)
-        tt("wu wj", "pre", T.pre[:, 0:M], T.wu[:, 15:C:16], WJ, Op.subtract)
+        tt("wu wj", "pre1", T.pre[:, M:2 * M], T.wu[:, 15:C:16], WJ, Op.subtract)
         tt("cd nb", "s2", T.s2[:, 0:M], T.cd[:, 15:C:16], T.nb[:, 0:M], Op.subtract)
         for m in range(0, 4):
             scan_b(m), scan_a(m)
-        cp("landl", "kb", T.kb[:, 0:M], BU)
-        scan_b(4), scan_a(4)
-        tt("kb kc", "kb", T.kb[:, 0:M], T.kb[:, 0:M], T.kc[:, 0:M], Op.add)
-        act("s2 kq", "s3", T.s3[:, 0:M], T.s2[:, 0:M], Act.Identity, bias=KQ, scale=2.0)
-        act("wj", "me2", T.me[:, 2 * M:3 * M], WJ)
-        act("wj", "me3", T.me[:, 3 * M:4 * M], WJ)
+        tt("landa kc", "kb", T.kb[:, 0:M], BF_, T.kc[:, 0:M], Op.add)
+        act("s2 kq cu2", "s3", T.s3[:], T.s2[:, 0:M].indirect(REP), Act.Identity, bias=KQ, scale=512.0)
+        act("accz " + keys("acc", range(M - 1)), "acs", T.acs[:, 0:M], T.acc[:, 0:M], scale=-256.0)
+        act("s3", "s3", T.s3[:, 0:4 * M], T.s3[:, 0:4 * M], Act.Identity, bias=512.0)
+        for k in (2, 3, 6, 7):
+            act("wj", "me%d" % k, pl(T.me, k, 1, M), WJ, Act.Identity, bias=255.0, scale=512.0)
         if r == 0:
             consts_late()
         for m in range(NB):
             act("key kb", "junk%d racc%d" % (m, m), pl(T.junk, m), T.key[:], Act.Sign, bias=T.kb[:, mine + m:mine + m + 1], scale=-1.0,
-                accum_out=T.racc[:, 8 * r + m:8 * r + m + 1])
+                accum_out=T.racc[:, 2 * r + half, m:m + 1])
         order("g", keys("racc", range(NB)).split(), [])
-        send(peer, T.landr[:, 8 * r:8 * r + NB], T.racc[:, 8 * r:8 * r + NB], T.sem["ar%d" % r])
+        send(peer, T.racc[:, 2 * r + half, 0:NB], T.racc[:, 2 * r + half, 0:NB], T.sem["ar%d" % r])
         wrote["landr"] = [("ar%d" % r, ne)]
         act("arow landl", "alpha", T.alpha[:], T.arow[:].indirect(COLB))
-        for m in range(5, M - 1):
+        for m in range(4, M - 1):
             scan_b(m), scan_a(m)
         scan_b(M - 1)
-        tt("s3 accz " + keys("acc", range(M - 1)), "pt", T.pt[:, 0:M], T.s3[:, 0:M], T.acc[:, 0:M], Op.subtract)
+        tt("s3 acs cu2", "pt", T.pt[:], T.acs[:, 0:M].indirect(REP), T.s3[:], Op.add)
         scan_a(M - 1)
         OA, OB = keys("oa", range(M)), keys("ob", range(M))
         up = slice(C + 1, (M - 1) * (W - 16) + C + 2, W - 16)
-        dn = slice(W - 1, M * W, W)
-        tt(OB + " pre", "dd2", T.dd[:, 2 * M:3 * M], T.pre[:, 0:M], T.ob[:, dn], Op.subtract)
-        tt(OB + " wj", "dd3", T.dd[:, 3 * M:4 * M], T.ob[:, up], WJ, Op.subtract)
-        ts(OA + " kl", "dd0", T.dd[:, 0:M], T.oa[:, dn], -1.0, KL, Op.mult, Op.add)
-        tt(OA + " j1", "dd1", T.dd[:, M:2 * M], T.oa[:, up], T.j1[:, 0:M], Op.subtract)
-        ts("pt oddz", "odd", T.odd[:, 0:M], T.pt[:, 0:M], 1, 1, Op.arith_shift_right, Op.bitwise_and)
-        ts("dd0 dd1 dd2 dd3 ddz", "dc", T.dc[:], T.dd[:], -0.5, 0.5, Op.max, Op.min)
-        ME = "me0 me1 me2 me3"
-        tt("odd dc cu2", "do", T.do[:], T.odd[:].indirect(REP), T.dc[:], Op.mult)
-        tt("dc " + ME, "ds", T.ds[:, 0:4 * M], T.dc[:, 0:4 * M], T.me[:, 0:4 * M], Op.add)
-        tt("do " + ME, "l81", T.l8[:, 4 * M:8 * M], T.do[:, 0:4 * M], T.me[:, 0:4 * M], Op.add)
-        tt("do ds", "l80", T.l8[:, 0:4 * M], T.ds[:, 0:4 * M], T.do[:, 0:4 * M], Op.subtract)
-        ts("l80 l81", "li", T.li[:], T.l8[:], 512.0, 255.0, Op.mult, Op.add)
+        upb = slice(M * W + up.start, M * W + up.stop, up.step)
+        tt(OB + " wj", "dd2", T.dd[:, 3 * M:4 * M], T.oo[:, upb], WJ, Op.subtract)
+        ts("pt", "fl", T.fl[:], T.pt[:], 512, None, Op.bitwise_and)
+        tt(OA + " " + OB + " pre0 pre1", "dd1", T.dd[:, M:3 * M], T.pre[:], T.oo[:, W - 1:2 * M * W:W], Op.subtract)
+        tt(OA + " j1", "dd0", T.dd[:, 0:M], T.oo[:, up], T.j1[:, 0:M], Op.subtract)
+        for k in range(2):
+            tt("dd0 dd1 dd2 fl", "d8%d" % k, pl(T.d8, k, 1, 4 * M), pl(T.fl, k, 1, 4 * M), T.dd[:], Op.mult)
+        ts("d80 d81", "dc", T.dc[:], T.d8[:], -256.0, 256.0, Op.max, Op.min)
+        tt("dc " + keys("me", range(8)), "li", T.li[:], T.dc[:], T.me[:], Op.add)
         ts("li", "lj", T.lj[:], T.li[:], 255, None, Op.bitwise_and)
         cp("lj", "lu", T.lu[:], T.lj[:])
         act("alpha lu", "lk1", pl(T.lk, 1), T.alpha[:].indirect(T.lu[:, 3 * M:4 * M]))
@@ -382,10 +401,10 @@ def rank_program(g, core, T, topo):
             act("xa%d lb" % t, "bd%d" % t, pl(T.bd, 2 * t, 2), pl(T.xa, t).indirect(T.lb[:]))
 
         def low(t):
-            tt("xa%d lu bd%d" % (t, t), "lo%d" % t, pl(T.lo, t), pl(T.xa, t).indirect(T.lu[:, 0:M]), pl(T.bd, 2 * t), Op.max)
+            tt("xa%d lu bd%d" % (t, t), "lo%d" % t, pl(T.lo, t), pl(T.xa, t).indirect(T.lu[:, M:2 * M]), pl(T.bd, 2 * t), Op.max)
 
         def high(t):
-            tt("xa%d lu bd%d" % (t, t), "hi%d" % t, pl(T.hi, t), pl(T.xa, t).indirect(T.lu[:, M:2 * M]), pl(T.bd, 2 * t + 1), Op.min)
+            tt("xa%d lu bd%d" % (t, t), "hi%d" % t, pl(T.hi, t), pl(T.xa, t).indirect(T.lu[:, 0:M]), pl(T.bd, 2 * t + 1), Op.min)
 
         def add(t, n):
             ks = range(t, t + n)
@@ -395,13 +414,13 @@ def rank_program(g, core, T, topo):
             ks = range(t, t + n)
             tt(keys("vv", ks) + " " + keys("xa", ks), keys("x1", ks), pl(T.x1, t, n), pl(T.vv, t, n), pl(T.xa, t, n), Op.subtract)
 
-        part = ((0, A, 0, MA), (4 * A, B, 5 * MA, MB))
-        own = (T.lf[:, 4 * MA:5 * MA], T.lf[:, 5 * MA + 4 * MB:5 * M])
+        part = ((0, A, 0, MA), (4 * A, B, 4 * MA, MB))
+        own = (T.lf[:, 4 * M:4 * M + MA], T.lf[:, 4 * M + MA:5 * M])
 
         def relist(i):
             o, w = part[i][0:2]
             for k in range(4):
-                act("lr0 lr1 own%d" % i, "lp%d%d" % (i, k), T.lp[:, o + k * w:o + (k + 1) * w], pl(T.lr, k).indirect(own[i]))
+                act("lr0 lr1 own", "lp%d%d" % (i, k), T.lp[:, o + k * w:o + (k + 1) * w], pl(T.lr, k).indirect(own[i]))
 
         def lists(i):
             o, w, c, n = part[i]
@@ -410,63 +429,68 @@ def rank_program(g, core, T, topo):
 
         far(0), far(1), far(2)
         cp("alpha lu", "lr1", pl(T.lr, 2, 2), T.alpha[:].indirect(T.lu[:, 6 * M:8 * M]))
-        ts(keys("racc", range(NB)), "ru0", T.ru[:, mine:mine + NB], T.racc[:, 8 * r:8 * r + NB], -0.5, (C - 1) / 2.0, Op.mult, Op.add)
-        low(0), high(0)
-        ts("landr", "ru1", T.ru[:, NB - mine:M - mine], T.landr[:, 8 * r:8 * r + NB], -0.5, (C - 1) / 2.0, Op.mult, Op.add)
-        low(1)
-        cp("arow ru0 ru1", "erow", T.erow[:].indirect(T.ru[:, 0:M]), T.arow[:])
-        far(3)
+        low(0), high(0), low(1)
+        ts("landr " + keys("racc", range(NB)), "ru", T.ru[:, 0:M], T.racc[:, 2 * r:2 * r + 2, 0:NB], -0.5, (C - 1) / 2.0, Op.mult, Op.add)
         high(1)
-        diag("erow", "d5", T.d5[:], T.erow[:], C)
+        cp("arow ru", "erow", T.erow[:].indirect(T.ru[:, 0:M]), T.arow[:])
+        far(3)
         add(0, 2)
-        ts("d5 k1", "own0", own[0], T.d5[:, 15:A:16], K1, -1.0, Op.mult, Op.add)
+        diag("erow", "d5", T.d5[:], T.erow[:], C)
+        sub(0, 2)
+        ts("d5 k1", "own", T.lf[:, 4 * M:5 * M], T.d5[:, 15:C:16], K1, -1.0, Op.mult, Op.add)
         relist(0)
-        ts("d5 k1", "own1", own[1], T.d5[:, A + 15:C:16], K1, -1.0, Op.mult, Op.add)
-        sub(0, 2), low(2), high(2)
+        low(2), high(2), low(3)
 
         def far2(i, t):
             o, w, c, n = part[i]
-            act("x1%d lf%d own%d" % (t, i, i), "be%d%d" % (i, t), T.be[:, 3 * (o + t * w):3 * (o + t * w + w)],
-                pl(T.x1, t).indirect(T.lf[:, c + 2 * n:c + 5 * n]))
+            act("x1%d lf%d" % (t, i), "be%d%d" % (i, t), T.be[:, 2 * (o + t * w):2 * (o + t * w + w)],
+                pl(T.x1, t).indirect(T.lf[:, c + 2 * n:c + 4 * n]))
+
+        def self0(t):
+            act("x1%d own" % t, "xs%d" % t, T.xs[:, t:4 * A:4], pl(T.x1, t).indirect(own[0]))
+
+        def self1(t):
+            act("x1%d own" % t, "xs%d" % (t + 4), T.xs[:, 4 * A + t * B:4 * A + (t + 1) * B], pl(T.x1, t).indirect(own[1]))
 
         def near2(i, t, k):
             o, w, c, n = part[i]
             buf, name = ((T.lo, "lo"), (T.hi, "hi"))[k]
-            tt("x1%d lf%d be%d%d" % (t, i, i, t), "%s%d" % (name, t + 4), pl(buf, t, 1, w), pl(T.x1, t).indirect(T.lf[:, c + k * n:c + (k + 1) * n]),
-               T.be[:, 3 * (o + t * w) + k * w:3 * (o + t * w) + (k + 1) * w], (Op.max, Op.min)[k])
+            tt("x1%d lf%d be%d%d" % (t, i, i, t), "%s%d" % (name, t + 4), pl(buf, t, 1, w) if i else buf[:, t:4 * A:4],
+               pl(T.x1, t).indirect(T.lf[:, c + (1 - k) * n:c + (2 - k) * n]),
+               T.be[:, 2 * (o + t * w) + k * w:2 * (o + t * w) + (k + 1) * w], (Op.max, Op.min)[k])
 
-        def add2(i, t):
-            w = part[i][1]
-            tt("lo%d lo%d hi%d hi%d" % (t + 4, t + 5, t + 4, t + 5), "vv%d vv%d" % (t + 4, t + 5), pl(T.vv, t, 2, w), pl(T.lo, t, 2, w), pl(T.hi, t, 2, w), Op.add)
+        def add2(t):
+            tt("lo%d lo%d hi%d hi%d" % (t + 4, t + 5, t + 4, t + 5), "vv%d vv%d" % (t + 4, t + 5), pl(T.vv, t, 2, B), pl(T.lo, t, 2, B), pl(T.hi, t, 2, B), Op.add)
 
-        def sub2(i, t):
-            o, w, c, n = part[i]
-            out, name = ((T.ft[:, t:4 * A:4], "ft"), (pl(T.x2, t, 1, B), "x2"))[i]
-            tt("vv%d be%d%d" % (t + 4, i, t), "%s%d" % (name, t), out, pl(T.vv, t, 1, w),
-               T.be[:, 3 * (o + t * w) + 2 * w:3 * (o + t * w + w)], Op.subtract)
-            if i:
-                act("x2%d" % t, "zx%d" % t, T.z64[:, t * C + A:(t + 1) * C], pl(T.x2, t, 1, B), scale=64.0)
+        def sub2(t):
+            tt("vv%d vv%d xs%d xs%d" % (t + 4, t + 5, t + 4, t + 5), "x2%d" % t, pl(T.x2, t, 2, B), pl(T.vv, t, 2, B),
+               T.xs[:, 4 * A + t * B:4 * A + (t + 2) * B], Op.subtract)
+            for k in (t, t + 1):
+                act("x2%d" % t, "zx%d" % k, T.z64[:, k * C + A:(k + 1) * C], pl(T.x2, k, 1, B), scale=64.0)
 
         lists(0)
-        far2(0, 0), far2(0, 1)
-        low(3), high(3), add(2, 2), near2(0, 0, 0), sub(2, 2)
-        far2(0, 2), far2(0, 3)
+        far2(0, 0), far2(0, 1), self0(0), self0(1)
+        high(3), add(2, 2), sub(2, 2)
+        far2(0, 2), far2(0, 3), self0(2), self0(3)
         relist(1)
-        near2(0, 0, 1), near2(0, 1, 0), near2(0, 1, 1), near2(0, 2, 0), add2(0, 0), near2(0, 2, 1), sub2(0, 0)
-        near2(0, 3, 0), near2(0, 3, 1), sub2(0, 1), add2(0, 2), sub2(0, 2), sub2(0, 3)
+        self1(0), self1(1), self1(2), self1(3)
+        for t in range(4):
+            near2(0, t, 0), near2(0, t, 1)
+        tt(keys("lo", range(4, 8)) + " " + keys("hi", range(4, 8)), keys("vv", range(4, 8)), T.vv[:, 0:4 * A], T.lo[:, 0:4 * A], T.hi[:, 0:4 * A], Op.add)
+        tt(keys("vv", range(4, 8)) + " " + keys("xs", range(4)), "ft0", T.ft[:, 0:4 * A], T.vv[:, 0:4 * A], T.xs[:, 0:4 * A], Op.subtract)
         f0, l0 = 128 * r, (R - 1 - r) * A
-        quant("ft " + keys("ft", range(4)), "qf", T.qf[:, f0:f0 + 128], T.sf[:, f0:f0 + 128], T.ft[:])
+        quant("ft ft0", "qf", T.qf[:, f0:f0 + 128], T.sf[:, f0:f0 + 128], T.ft[:])
         order("g", ["qf"], [])
         send(peer, T.ql[:, l0:l0 + A].bitcast(dt.uint8), T.qf[:, f0:f0 + A].bitcast(dt.uint8), T.sem["af%d" % r])
         send(peer, T.sl[:, l0:l0 + A], T.sf[:, f0:f0 + A], T.sem["af%d" % r])
         wrote["ql"] = [("af%d" % r, 2 * ne)]
         lists(1)
         far2(1, 0), far2(1, 1), far2(1, 2), far2(1, 3)
-        ts(keys("ft", range(4)), "f64", T.f64[:], T.ft[:, 0:4 * A], 64.0, None, Op.mult)
+        ts("ft0", "f64", T.f64[:], T.ft[:, 0:4 * A], 64.0, None, Op.mult)
         if r == 0:
             quant("vb", "qv", T.qv[:], T.sv[:], T.vb[:])
-        near2(1, 0, 0), near2(1, 0, 1), near2(1, 1, 0), near2(1, 1, 1), add2(1, 0), near2(1, 2, 0), sub2(1, 0)
-        near2(1, 2, 1), sub2(1, 1), near2(1, 3, 0), near2(1, 3, 1), add2(1, 2), sub2(1, 2), sub2(1, 3)
+        near2(1, 0, 0), near2(1, 0, 1), near2(1, 1, 0), near2(1, 1, 1), near2(1, 2, 0), add2(0)
+        near2(1, 2, 1), sub2(0), near2(1, 3, 0), near2(1, 3, 1), add2(2), sub2(2)
         for b in range(4):
             mm("w ql qlz", "pw%d" % b, T["pw%d" % b][:, 0:128], pl(T.qw, b, 1, 128), pl(T.sw, b, 1, 128),
                T.ql[:, l0:l0 + 128], T.sl[:, l0:l0 + 128])
@@ -475,9 +499,9 @@ def rank_program(g, core, T, topo):
         for t in range(4):
             src = pl(T.z64, t).indirect(T.ru[:, 0:M])
             if t < 2:
-                act("zx%d zh%d ru0 ru1" % (t, t), "xn%d" % t, T.xn[:, t:4 * C:4], src, scale=0.015625)
+                act("zx%d zh%d ru" % (t, t), "xn%d" % t, T.xn[:, t:4 * C:4], src, scale=0.015625)
             else:
-                ts("zx%d zh%d ru0 ru1" % (t, t), "xn%d" % t, T.xn[:, t:4 * C:4], src, 0.015625, None, Op.mult)
+                ts("zx%d zh%d ru" % (t, t), "xn%d" % t, T.xn[:, t:4 * C:4], src, 0.015625, None, Op.mult)
         quant(XN, "qx", T.qx[:], T.sx[:], T.xn[:])
 
     mm("qv qx", "pa", T.pa[:, 0:C], T.qv[:], T.sv[:], T.qx[:], T.sx[:])

from concourse.mybir import dt, AluOpType as Op, ActivationFunctionType as Act

C, A, R = 224, 96, 3
STEP = [4, 1, 2]
M = C // 16
MA = A // 16
B, MB = C - A, M - MA
NB = C // 32
W = C + 18
TINY = 2.0 ** -100

F8, U8, BF, F32, I32, U16 = "float8_e4m3fn_x4", "uint8", "bfloat16", "float32", "int32", "uint16"


def _sb(dtype, **cols):
    return {k: ("sbuf", [128, n], dtype) for k, n in cols.items()}


SCRATCH = {
    **_sb(F8, qu=128, qp=384, qv=128, qw=512, qx=C, ql=R * A + 128, qf=R * 128),
    **_sb(U8, su=128, sp=384, sv=128, sw=512, sx=C, sl=R * A + 128, sf=R * 128),
    **{k: ("psum", [128, 512], F32) for k in ("pa", "ph0", "ph1", "pw0", "pw1", "pw2", "pw3")},
    **_sb(BF, xn=4 * C, ub=512, vb=512, sendp=R * 16, landp=R * 16, senda=R * 16, landa=R * 16),
    **_sb(U16, sendl=R * 16, landl=R * 16), "racc": ("sbuf", [128, 2 * R, 8], F32),
    **_sb(I32, ci=66, pi=4), **_sb(U16, cu=74), **_sb(F32, col=16, cc=8, tmpc=32, cfr=16, j1=16, kj=16),
    **_sb(BF, one=C, r16=C, dg=4 * B, dgt=C, tri=NB * C, rs=4 * C, rs16=C, stl=C, stu=C, stv=C, za=2 * C + 2),
    **_sb(F32, ta=C, ca=8),
    **_sb(BF, df=M * C, mk=M * C, cn=M * C, bca=C, arow=C, bcb=C, brow=C, crow=C, alpha=C, erow=C, d1=C, d2=C, d3=C, d5=C),
    **_sb(U16, au=16, c4u=4 * M, ru=16),
    **_sb(BF, wu=C + 2, zb=2 * C + 2, ee=C, nu=C, cd=C, oo=2 * M * W, lk=2 * C, ld=2 * C, lr=4 * C, lp=4 * C, le=4 * C),
    "nm": ("sbuf", [128, M, W], BF),
    **_sb(F32, me=8 * M, wj=16, nb=16, acc=16, acs=16, s2=16, s3=8 * M, pre=2 * M, dd=4 * M, d8=8 * M, dc=8 * M),
    **_sb(I32, pt=8 * M, fl=8 * M, li=8 * M, lj=8 * M), **_sb(U16, lu=8 * M, lb=2 * M, lf=5 * M),
    **_sb(F32, ka=16, kk=16, ks=C, key=C, kc=16, kb=16), **_sb(BF, junk=NB * C),
    **_sb(BF, xp=4 * C, xs=4 * C, xa=4 * C, x1=4 * C, x2=4 * B, bd=8 * C, be=8 * C, lo=4 * C, hi=4 * C, vv=4 * C,
          ft=512, f64=4 * A, z64=4 * C),
    **_sb(F32, ys=C),
}
SEMAPHORES = ["ev", "es", "et", "eg", "lx", "lu", "lw", "lv", "sent", "st", "ap0", "ap1", "ap2", "al0", "al1", "al2",
              "aa0", "aa1", "aa2", "ar0", "ar1", "ar2", "af0", "af1", "af2"]


def rank_program(g, core, T, topo):
    rank = T.rank_of(core)
    if rank is None:
        return
    Q = {"v": g.vector, "s": g.scalar, "t": g.tensor, "g": g, "y": g.sync}
    names = {"v": "ev", "s": "es", "t": "et", "g": "eg"}
    count = {"v": 0, "s": 0, "t": 0, "g": 0}
    seen = {}
    wrote = {}
    read = {}

    def need(q, events):
        top = {}
        for name, n in events:
            top[name] = max(top.get(name, 0), n)
        for name, n in top.items():
            if seen.get((q, name), 0) < n:
                Q[q].wait_ge(T.sem[name], n)
                seen[(q, name)] = n

    def order(q, rd, wr):
        ev = []
        for k in rd:
            ev += wrote.get(k, [])
        for k in wr:
            ev += wrote.get(k, []) + read.get(k, [])
        need(q, ev)

    def op(q, rd, wr, call):
        rd, wr = rd.split(), wr.split()
        order(q, rd, wr)
        count[q] += 1
        call().then_inc(T.sem[names[q]], 1)
        e = (names[q], count[q])
        for k in rd:
            read.setdefault(k, []).append(e)
        for k in wr:
            wrote[k] = [e]
            read[k] = []

    def keys(name, ks):
        return " ".join("%s%d" % (name, k) for k in ks)

    def ts(rd, wr, out, in0, s1, s2, o0, o1=None):
        if o1 is None:
            op("v", rd, wr, lambda: g.vector.tensor_scalar(out, in0, s1, None, o0))
        else:
            op("v", rd, wr, lambda: g.vector.tensor_scalar(out, in0, s1, s2, o0, o1))

    def tt(rd, wr, out, a, b, o):
        op("v", rd, wr, lambda: g.vector.tensor_tensor(out, a, b, o))

    def cp(rd, wr, out, a):
        op("v", rd, wr, lambda: g.vector.tensor_copy(out, a))

    def ms(wr, out, c):
        op("v", "", wr, lambda: g.vector.memset(out, c))

    def scan(rd, wr, out, a, b, init, o0, o1):
        op("v", rd, wr, lambda: g.vector.tensor_tensor_scan(out, a, b, init, o0, o1))

    def turn(rd, wr, out, a):
        op("v", rd, wr, lambda: g.vector.transpose(out, a))

    def act(rd, wr, out, a, f=Act.Copy, **kw):
        op("s", rd, wr, lambda: g.scalar.activation(out, a, f, **kw))

    def fill(wr, out, n, c):
        act("one", wr, out, T.one[:, 0:n], Act.Identity, bias=c, scale=0.0)

    def iota(wr, out, pat, base, cm, small=False):
        if small:
            op("g", "", wr, lambda: g.iota(out, pat, base, cm, allow_small_or_imprecise_dtypes=True))
        else:
            op("g", "", wr, lambda: g.iota(out, pat, base, cm))

    def quant(rd, wr, q, s, a):
        op("v", rd, wr, lambda: g.vector.quantize_mx(q, s, a))

    def mm(rd, wr, out, lq, ls, rq, rs):
        op("t", rd, wr, lambda: g.tensor.matmul_mx(out, lq, ls, rq, rs, True, True))

    def diag(rd, wr, out, row, n):
        scan(rd + " dg", wr, out, T.dg[:, 0:n], row, 0.0, Op.mult, Op.max)

    def pl(buf, t, n=1, w=C):
        return buf[:, t * w:(t + n) * w]

    g.scalar.dma_start(T.ub[:], T.u[:]).then_inc(T.sem.lu, 16)
    g.sync.dma_start(T.xn[:], T.x[:]).then_inc(T.sem.lx, 16)
    g.sync.dma_start(T.qw[:].bitcast(dt.uint8), T.wc[:]).then_inc(T.sem.lw, 16)
    g.sync.dma_start(T.sw[:], T.ws[:]).then_inc(T.sem.lw, 16)
    g.sync.dma_start(T.vb[:], T.v[:]).then_inc(T.sem.lv, 16)
    XN = keys("xn", range(4))
    for k in XN.split():
        wrote[k] = [("lx", 16)]
    wrote["ub"], wrote["w"], wrote["vb"] = [("lu", 16)], [("lw", 32)], [("lv", 16)]

    iota("pi0", T.pi[:, 0:1], [[0, 1]], 0, 1)
    iota("cc", T.cc[:], [[32, 8]], 1, 0, True)
    iota("one", T.one[:], [[1, C]], 1, 0, True)
    iota("ci0", T.ci[:, 0:8], [[16, 8]], 0, 0)
    iota("ci1", T.ci[:, 8:24], [[16, 2], [32, 4], [0, 2]], 0, 0)
    iota("r16", T.r16[:], [[0, M], [1, 16]], 0, 0, True)
    iota("ci2", T.ci[:, 24:38], [[1, NB], [NB, 2]], 0, 0)
    iota("ci3", T.ci[:, 38:52], [[1, M]], 0, 0)
    iota("ci4", T.ci[:, 52:66], [[C, NB], [NB * C, 2]], C - 1, 0)
    iota("j1", T.j1[:], [[16, 16]], 1, 0, True)
    iota("tmpc", T.tmpc[:, 0:8], [[2, 8]], 0, 0, True)
    iota("wuz", T.wu[:, C:C + 2], [[0, 2]], 0, 0, True)
    iota("accz", T.acc[:], [[0, 16]], 0, 0, True)
    iota("za3 za4", T.za[:, C + 1:C + 3], [[3, 2]], 1, 0, True)
    iota("zc3 zc4", T.zb[:, C + 1:C + 3], [[3, 2]], 1, 0, True)
    iota("zc5", T.zb[:, 0:1], [[0, 1]], 0, 0, True)
    for m in range(M):
        iota("nmz%d" % m, T.nm[:, m, C - 16 * m:C + 2 - 16 * m], [[0, 2]], 4, 0, True)
    P32, Q16 = T.col[:, 0:1], T.col[:, 1:2]
    K1, K4, KN, KL, KQ, KS = [T.col[:, k:k + 1] for k in range(3, 9)]
    ms("ft", T.ft[:, 4 * A:512], 0.0)
    ts("pi0", "pi1", T.pi[:, 1:2], T.pi[:, 0:1], 31, None, Op.bitwise_and)
    ts("pi0", "pi2", T.pi[:, 2:3], T.pi[:, 0:1], 15, None, Op.bitwise_and)
    cp("pi1 pi2", "colq", T.col[:, 0:2], T.pi[:, 1:3])
    ts("cc colq", "cc", T.cc[:], T.cc[:], P32, None, Op.add)
    ts("colq", "col2", T.col[:, 2:3], Q16, 15.0, -16.0, Op.is_equal, Op.mult)
    ts("colq", "k1", K1, Q16, 15.0, 255.0, Op.is_equal, Op.mult)
    for k in range(4):
        act("one", "rs%d" % k, pl(T.rs, k), T.one[:], Act.Sign, bias=-1.0)

    def tri(b):
        ts("one cc", "tri%d" % b, pl(T.tri, b), T.one[:], T.cc[:, b:b + 1], TINY, Op.is_le, Op.mult)

    tri(0)
    cp("ci0 ci1", "cu0", T.cu[:, 0:24], T.ci[:, 0:24])
    ts("col2 colq", "col2", T.col[:, 2:3], T.col[:, 2:3], Q16, 1.0, Op.add, Op.add)
    ts("k1", "k1", K1, K1, 1.0, 1.0 / 256, Op.add, Op.mult)
    for b in range(1, 5):
        tri(b)
    quant("ub", "qu", T.qu[:], T.su[:], T.ub[:])
    quant(XN, "qx", T.qx[:], T.sx[:], T.xn[:])
    op("v", "qu cu0", "qp", lambda: g.vector.tensor_copy(T.qp[:].bitcast(dt.uint32), T.qu[:].bitcast(dt.uint32).indirect(T.cu[:, 0:24])))
    act("qu cu0", "sp", T.sp[:], T.su[:].indirect(T.cu[:, 0:24]))

    def consts_rows():
        ts("r16 colq", "dg", T.dg[:, 0:C], T.r16[:], Q16, None, Op.not_equal)
        ts("r16 col2", "dgt", T.dgt[:], T.r16[:], T.col[:, 2:3], 255.0, Op.is_equal, Op.mult)
        cp("ci2 ci3 ci4", "cu1", T.cu[:, 24:66], T.ci[:, 24:66])
        tt("dg dgt", "dg", T.dg[:, 0:C], T.dg[:, 0:C], T.dgt[:], Op.add)

    def consts_scalar():
        act("cc", "cfr0", T.cfr[:, 0:NB], T.cc[:, 0:NB], scale=-1.0 / 256)
        act("cc", "cfr1", T.cfr[:, NB:M], T.cc[:, 0:NB], scale=-1.0 / 256)
        act("k1", "k4", K4, K1, scale=4.0)
        act("colq", "ks0", KS, Q16, scale=1.0 / 512)
        act("k1", "kn", KN, K1, scale=-512.0)
        act("colq", "kl", KL, Q16, Act.Identity, bias=15.0 / 512, scale=-1.0 / 512)
        act("colq", "kq", KQ, Q16, Act.Identity, bias=260.0 * 256, scale=512.0)
        act("j1 ks0", "j1", T.j1[:], T.j1[:], Act.Identity, bias=KS, scale=1.0 / 512)
        act("colq", "tq", T.tmpc[:, 24:25], Q16, Act.Identity, bias=1.0)
        act("colq", "tn", T.tmpc[:, 25:26], Q16, Act.Identity, bias=1.0, scale=-1.0)
        act("j1", "kj", T.kj[:], T.j1[:], scale=-2.0)

    def consts_masks():
        act("r16 tq", "stv", T.stv[:], T.r16[:], Act.Relu, bias=T.tmpc[:, 24:25], scale=-1.0)
        act("r16 tn", "stl", T.stl[:], T.r16[:], Act.Relu, bias=T.tmpc[:, 25:26])
        act("stv", "stu", T.stu[:], T.stv[:], scale=-1.0)
        act("r16", "rs16", T.rs16[:], T.r16[:], Act.Sign)
        fill("za0", T.za[:, 0:C], C, -1.0 / 512)
        fill("za1", T.za[:, C:C + 1], 1, C / 512.0)
        fill("za2", T.za[:, C + 3:2 * C + 2], C - 1, 1.0 / 512)

    def consts_late():
        act("one kl", "pre0", T.pre[:, 0:M], T.one[:, 0:M], Act.Identity, bias=KL, scale=0.0)
        for k in (0, 1, 4, 5):
            act("j1", "me%d" % k, pl(T.me, k, 1, M), T.j1[:, 0:M], Act.Identity, bias=255.0, scale=512.0)
        act("dg", "dgb", T.dg[:, C:2 * C], T.dg[:, 0:C])
        act("dg", "dgc", T.dg[:, 2 * C:4 * B], T.dg[:, 0:4 * B - 2 * C])

    def consts_lists():
        ts("tmpc colq", "tmpc", T.tmpc[:, 0:8], T.tmpc[:, 0:8], Q16, None, Op.add)
        ts("tmpc", "tmpd", T.tmpc[:, 8:16], T.tmpc[:, 0:8], float(M), -float(M), Op.is_ge, Op.mult)
        tt("tmpc tmpd", "tmpe", T.tmpc[:, 16:24], T.tmpc[:, 0:8], T.tmpc[:, 8:16], Op.add)
        cp("tmpe", "cu2", T.cu[:, 66:74], T.tmpc[:, 16:24])

    SPREAD, SPREAD16, ENDS, REP = T.cu[:, 24:38], T.cu[:, 38:52], T.cu[:, 52:66], T.cu[:, 66:73]
    writes = [0]

    def send(peer, out, src, sem):
        rid, pid = topo.addr(peer, core)
        g.remote_dma(out, src, sem, T.sem.sent, pid, rid, topo.mask(core, peer))
        writes[0] += len(topo.engines(core, peer))

    for r in range(R):
        peer = T.cores[rank ^ STEP[r]]
        half = 1 if rank & STEP[r] else 0
        mine = NB * half
        ne = len(topo.engines(peer, core))
        for k, (ps, n) in enumerate(((T.pa, "pa"), (T.ph0, "ph0"), (T.ph1, "ph1"))):
            mm("qp sp qx", n, ps[:, 0:C], pl(T.qp, k, 1, 128), pl(T.sp, k, 1, 128), T.qx[:], T.sx[:])
        if r == 0:
            tri(5), tri(6)
        turn("pa", "ta0", T.ta[:, 0:64], T.pa[:, 0:64])
        turn("pa", "ta1", T.ta[:, 64:C], T.pa[:, 64:C])
        if r == 0:
            consts_rows()
        for b in (NB - 1, NB - 2):
            ts("ta1", "ph1 df%d" % (NB + b), pl(T.df, NB + b), T.ph1[:, 0:C], -1.0, T.ta[:, 32 * b + 16:32 * b + 17], Op.mult, Op.add)
        for k in range(M - 2):
            h, b = k // NB, k % NB
            act("ph%d ta%d" % (h, b > 1), "df%d" % k, pl(T.df, k), (T.ph0, T.ph1)[h][:, 0:C], Act.Identity,
                bias=T.ta[:, 32 * b + 16 * h:32 * b + 16 * h + 1], scale=-1.0)

        def compare(h, b0, b1):
            k, ks = h * NB + b0, range(h * NB + b0, h * NB + b1)
            tt(keys("df", ks) + " " + keys("tri", range(b0, b1)), keys("mk", ks), pl(T.mk, k, b1 - b0), pl(T.df, k, b1 - b0),
               pl(T.tri, b0, b1 - b0), Op.is_lt)

        def total(h, b0, b1):
            k, ks = h * NB + b0, range(h * NB + b0, h * NB + b1)
            scan(keys("rs", range(4)) + " " + keys("mk", ks), keys("cn", ks), pl(T.cn, k, b1 - b0), pl(T.rs, 0, b1 - b0),
                 pl(T.mk, k, b1 - b0), 0.0, Op.mult, Op.add)

        sp_, lp_ = T.sendp[:, 16 * r:16 * r + M], T.landp[:, 16 * r:16 * r + M]
        COL, COLB, AU = T.sendl[:, 16 * r:16 * r + M], T.landl[:, 16 * r:16 * r + M], T.au[:, 0:M]
        AF, BF_ = T.senda[:, 16 * r:16 * r + M], T.landa[:, 16 * r:16 * r + M]
        compare(0, 0, 1), compare(0, 1, 3), compare(0, 3, 5)
        total(0, 0, 3)
        compare(0, 5, 7), compare(1, 0, 2)
        total(0, 3, 5)
        compare(1, 2, 5), compare(1, 5, 7)
        for k in range(6):
            act("mk%d" % (5 + k), "junk%d ca%d" % (k, k), pl(T.junk, k), pl(T.mk, 5 + k), Act.Identity, accum_out=T.ca[:, k:k + 1])
        act(keys("ca", range(6)), keys("cn", range(5, 11)), T.cn[:, 6 * C - 1:11 * C:C], T.ca[:, 0:6])
        total(1, 4, 7)
        act(keys("cn", range(M)), "sendp", sp_, T.cn[:, C - 1:M * C:C])
        order("g", ["sendp"], [])
        send(peer, lp_, sp_, T.sem["ap%d" % r])
        wrote["landp"] = [("ap%d" % r, ne)]
        if r == 0:
            consts_scalar()

        def planes(ts_):
            for t in ts_:
                act("xn%d" % t, "xp%d" % t, pl(T.xp, t), T.xn[:, t:4 * C:4])

        cp(keys("cn", range(M)) + " cu1", "bca", T.bca[:], T.cn[:].indirect(ENDS))
        if r > 0:
            planes((0, 1))
        tt("sendp cfr0 cfr1", "ka", T.ka[:, 0:M], sp_, T.cfr[:, 0:M], Op.add)
        turn("bca", "arow", T.arow[:], T.bca[:])
        diag("arow", "d1", T.d1[:], T.arow[:], C)
        ts("d1 k1", "au", AU, T.d1[:, 15:C:16], K1, -1.0, Op.mult, Op.add)
        cp("one au", "crow", T.crow[:].indirect(AU), T.one[:])
        act("d1 k1", "af", AF, T.d1[:, 15:C:16], scale=K1)
        if r == 0:
            consts_masks()
        else:
            planes((2, 3))
        order("g", ["af"], [])
        send(peer, BF_, AF, T.sem["aa%d" % r])
        wrote["landa"] = [("aa%d" % r, ne)]
        tt("af kj", "kc", T.kc[:, 0:M], AF, T.kj[:, 0:M], Op.add)
        diag("crow", "d2", T.d2[:], T.crow[:], C)
        ts("d2 k1", "colu", COL, T.d2[:, 15:C:16], K1, -1.0, Op.mult, Op.add)
        order("g", ["colu"], [])
        send(peer, COLB, COL, T.sem["al%d" % r])
        wrote["landl"] = [("al%d" % r, ne)]
        for t in range(4):
            if r == 0:
                ts("d2 k4", "c4u%d" % t, pl(T.c4u, t, 1, M), T.d2[:, 15:C:16], K4, t - 4.0, Op.mult, Op.add)
                act(XN + " c4u%d" % t, "xa%d" % t, pl(T.xa, t), T.xn[:].indirect(pl(T.c4u, t, 1, M)))
            else:
                act("xp%d colu" % t, "xa%d" % t, pl(T.xa, t), pl(T.xp, t).indirect(COL))
        if r == 0:
            quant(XN, "qlz", T.ql[:, R * A:R * A + 128], T.sl[:, R * A:R * A + 128], T.xn[:, 0:512])
            consts_lists()
        cp("landp cu1", "bcb", T.bcb[:], lp_.indirect(SPREAD))
        tt("landp ka", "kk", T.kk[:, 0:M], lp_, T.ka[:, 0:M], Op.add)
        act("kk cu1", "ks", T.ks[:], T.kk[:, 0:M].indirect(SPREAD))
        turn("bcb", "brow", T.brow[:], T.bcb[:])
        ts("brow colu", "wu", T.wu[:, 0:C], T.brow[:].indirect(COL), 1.0 / 512, None, Op.mult)
        diag("wu", "d3", T.d3[:], T.wu[:, 0:C], C)
        WJ = T.wj[:, 0:M]
        tt("wu wuz", "zb0", T.zb[:, 1:C + 1], T.wu[:, 0:C], T.wu[:, 1:C + 1], Op.subtract)
        act("d3 k1", "wj", WJ, T.d3[:, 15:C:16], scale=K1)
        act("d3 kn", "nb", T.nb[:, 0:M], T.d3[:, 15:C:16], scale=KN)

        def masks(m):
            if m < M - 1:
                act("wu wj accz", "nmu%d acc%d" % (m, m), T.nm[:, m, 16:C - 16 * m], T.wu[:, 16 * m + 16:C], Act.Sign,
                    bias=T.wj[:, m:m + 1], scale=-1.0, accum_out=T.acc[:, m:m + 1])
            if m > 0:
                act("wu nb", "nml%d" % m, T.nm[:, m, C + 2 - 16 * m:C + 2], T.wu[:, 0:16 * m], Act.Relu,
                    bias=T.nb[:, m:m + 1], scale=512.0)

        masks(0), masks(1)
        tt("wj wu cu1", "ee", T.ee[:], WJ.indirect(SPREAD16), T.wu[:, 0:C], Op.subtract)
        turn("ks", "key", T.key[:], T.ks[:])
        act("zb0", "zb1", T.zb[:, C + 3:2 * C + 2], T.zb[:, 1:C], scale=-1.0)
        tt("ee stu", "nu", T.nu[:], T.ee[:], T.stu[:], Op.is_lt)
        tt("ee stl", "ndl", T.nm[:, :, C + 2:W], T.ee[:], T.stl[:], Op.is_le)
        masks(2)
        act("nu", "ndu", T.nm[:, :, 0:16], T.nu[:], scale=-1.0)
        for m in range(3, M):
            masks(m)

        def scan_a(m):
            scan("nmu%d nml%d nmz%d ndl ndu " % (m, m, m) + keys("za", range(5)), "oa%d" % m, pl(T.oo, m, 1, W),
                 T.za[:, 16 * m:16 * m + W], T.nm[:, m, :], 4.0, Op.add, Op.min)

        def scan_b(m):
            scan("nmu%d nml%d nmz%d ndl ndu zb0 zb1 zc3 zc4 zc5" % (m, m, m), "ob%d" % m, pl(T.oo, M + m, 1, W),
                 T.zb[:, 16 * m:16 * m + W], T.nm[:, m, :], 4.0, Op.add, Op.min)

        scan("nu rs16", "cd", T.cd[:], T.rs16[:], T.nu[:], 0.0, Op.mult, Op.add)
        tt("wu wj", "pre1", T.pre[:, M:2 * M], T.wu[:, 15:C:16], WJ, Op.subtract)
        tt("cd nb", "s2", T.s2[:, 0:M], T.cd[:, 15:C:16], T.nb[:, 0:M], Op.subtract)
        for m in range(0, 4):
            scan_b(m), scan_a(m)
        tt("landa kc", "kb", T.kb[:, 0:M], BF_, T.kc[:, 0:M], Op.add)
        act("s2 kq cu2", "s3", T.s3[:], T.s2[:, 0:M].indirect(REP), Act.Identity, bias=KQ, scale=512.0)
        act("accz " + keys("acc", range(M - 1)), "acs", T.acs[:, 0:M], T.acc[:, 0:M], scale=-256.0)
        act("s3", "s3", T.s3[:, 0:4 * M], T.s3[:, 0:4 * M], Act.Identity, bias=512.0)
        for k in (2, 3, 6, 7):
            act("wj", "me%d" % k, pl(T.me, k, 1, M), WJ, Act.Identity, bias=255.0, scale=512.0)
        if r == 0:
            consts_late()
        for m in range(NB):
            act("key kb", "junk%d racc%d" % (m, m), pl(T.junk, m), T.key[:], Act.Sign, bias=T.kb[:, mine + m:mine + m + 1], scale=-1.0,
                accum_out=T.racc[:, 2 * r + half, m:m + 1])
        order("g", keys("racc", range(NB)).split(), [])
        send(peer, T.racc[:, 2 * r + half, 0:NB], T.racc[:, 2 * r + half, 0:NB], T.sem["ar%d" % r])
        wrote["landr"] = [("ar%d" % r, ne)]
        act("arow landl", "alpha", T.alpha[:], T.arow[:].indirect(COLB))
        for m in range(4, M - 1):
            scan_b(m), scan_a(m)
        scan_b(M - 1)
        tt("s3 acs cu2", "pt", T.pt[:], T.acs[:, 0:M].indirect(REP), T.s3[:], Op.add)
        scan_a(M - 1)
        OA, OB = keys("oa", range(M)), keys("ob", range(M))
        up = slice(C + 1, (M - 1) * (W - 16) + C + 2, W - 16)
        upb = slice(M * W + up.start, M * W + up.stop, up.step)
        tt(OB + " wj", "dd2", T.dd[:, 3 * M:4 * M], T.oo[:, upb], WJ, Op.subtract)
        ts("pt", "fl", T.fl[:], T.pt[:], 512, None, Op.bitwise_and)
        tt(OA + " " + OB + " pre0 pre1", "dd1", T.dd[:, M:3 * M], T.pre[:], T.oo[:, W - 1:2 * M * W:W], Op.subtract)
        tt(OA + " j1", "dd0", T.dd[:, 0:M], T.oo[:, up], T.j1[:, 0:M], Op.subtract)
        for k in range(2):
            tt("dd0 dd1 dd2 fl", "d8%d" % k, pl(T.d8, k, 1, 4 * M), pl(T.fl, k, 1, 4 * M), T.dd[:], Op.mult)
        ts("d80 d81", "dc", T.dc[:], T.d8[:], -256.0, 256.0, Op.max, Op.min)
        tt("dc " + keys("me", range(8)), "li", T.li[:], T.dc[:], T.me[:], Op.add)
        ts("li", "lj", T.lj[:], T.li[:], 255, None, Op.bitwise_and)
        cp("lj", "lu", T.lu[:], T.lj[:])
        act("alpha lu", "lk1", pl(T.lk, 1), T.alpha[:].indirect(T.lu[:, 3 * M:4 * M]))
        cp("alpha lu", "lk0", pl(T.lk, 0), T.alpha[:].indirect(T.lu[:, 2 * M:3 * M]))
        act("one lu", "lr0", pl(T.lr, 0, 2), T.one[:].indirect(T.lu[:, 4 * M:6 * M]))
        diag("lk0 lk1 dgb", "ld", T.ld[:], T.lk[:], 2 * C)
        ts("ld k1", "lb", T.lb[:], T.ld[:, 15:2 * C:16], K1, -1.0, Op.mult, Op.add)

        def far(t):
            act("xa%d lb" % t, "bd%d" % t, pl(T.bd, 2 * t, 2), pl(T.xa, t).indirect(T.lb[:]))

        def low(t):
            tt("xa%d lu bd%d" % (t, t), "lo%d" % t, pl(T.lo, t), pl(T.xa, t).indirect(T.lu[:, M:2 * M]), pl(T.bd, 2 * t), Op.max)

        def high(t):
            tt("xa%d lu bd%d" % (t, t), "hi%d" % t, pl(T.hi, t), pl(T.xa, t).indirect(T.lu[:, 0:M]), pl(T.bd, 2 * t + 1), Op.min)

        def add(t, n):
            ks = range(t, t + n)
            tt(keys("lo", ks) + " " + keys("hi", ks), keys("vv", ks), pl(T.vv, t, n), pl(T.lo, t, n), pl(T.hi, t, n), Op.add)

        def sub(t, n):
            ks = range(t, t + n)
            tt(keys("vv", ks) + " " + keys("xa", ks), keys("x1", ks), pl(T.x1, t, n), pl(T.vv, t, n), pl(T.xa, t, n), Op.subtract)

        part = ((0, A, 0, MA), (4 * A, B, 4 * MA, MB))
        own = (T.lf[:, 4 * M:4 * M + MA], T.lf[:, 4 * M + MA:5 * M])

        def relist(i):
            o, w = part[i][0:2]
            for k in range(4):
                act("lr0 lr1 own", "lp%d%d" % (i, k), T.lp[:, o + k * w:o + (k + 1) * w], pl(T.lr, k).indirect(own[i]))

        def lists(i):
            o, w, c, n = part[i]
            diag(keys("lp%d" % i, range(4)) + " dgb dgc", "le%d" % i, T.le[:, o:o + 4 * w], T.lp[:, o:o + 4 * w], 4 * w)
            ts("le%d k1" % i, "lf%d" % i, T.lf[:, c:c + 4 * n], T.le[:, o + 15:o + 4 * w:16], K1, -1.0, Op.mult, Op.add)

        far(0), far(1), far(2)
        cp("alpha lu", "lr1", pl(T.lr, 2, 2), T.alpha[:].indirect(T.lu[:, 6 * M:8 * M]))
        low(0), high(0), low(1)
        ts("landr " + keys("racc", range(NB)), "ru", T.ru[:, 0:M], T.racc[:, 2 * r:2 * r + 2, 0:NB], -0.5, (C - 1) / 2.0, Op.mult, Op.add)
        high(1)
        cp("arow ru", "erow", T.erow[:].indirect(T.ru[:, 0:M]), T.arow[:])
        far(3)
        add(0, 2)
        diag("erow", "d5", T.d5[:], T.erow[:], C)
        sub(0, 2)
        ts("d5 k1", "own", T.lf[:, 4 * M:5 * M], T.d5[:, 15:C:16], K1, -1.0, Op.mult, Op.add)
        relist(0)
        low(2), high(2), low(3)

        def far2(i, t):
            o, w, c, n = part[i]
            act("x1%d lf%d" % (t, i), "be%d%d" % (i, t), T.be[:, 2 * (o + t * w):2 * (o + t * w + w)],
                pl(T.x1, t).indirect(T.lf[:, c + 2 * n:c + 4 * n]))

        def self0(t):
            act("x1%d own" % t, "xs%d" % t, T.xs[:, t:4 * A:4], pl(T.x1, t).indirect(own[0]))

        def self1(t):
            act("x1%d own" % t, "xs%d" % (t + 4), T.xs[:, 4 * A + t * B:4 * A + (t + 1) * B], pl(T.x1, t).indirect(own[1]))

        def near2(i, t, k):
            o, w, c, n = part[i]
            buf, name = ((T.lo, "lo"), (T.hi, "hi"))[k]
            tt("x1%d lf%d be%d%d" % (t, i, i, t), "%s%d" % (name, t + 4), pl(buf, t, 1, w) if i else buf[:, t:4 * A:4],
               pl(T.x1, t).indirect(T.lf[:, c + (1 - k) * n:c + (2 - k) * n]),
               T.be[:, 2 * (o + t * w) + k * w:2 * (o + t * w) + (k + 1) * w], (Op.max, Op.min)[k])

        def add2(t):
            tt("lo%d lo%d hi%d hi%d" % (t + 4, t + 5, t + 4, t + 5), "vv%d vv%d" % (t + 4, t + 5), pl(T.vv, t, 2, B), pl(T.lo, t, 2, B), pl(T.hi, t, 2, B), Op.add)

        def sub2(t):
            tt("vv%d vv%d xs%d xs%d" % (t + 4, t + 5, t + 4, t + 5), "x2%d" % t, pl(T.x2, t, 2, B), pl(T.vv, t, 2, B),
               T.xs[:, 4 * A + t * B:4 * A + (t + 2) * B], Op.subtract)
            for k in (t, t + 1):
                act("x2%d" % t, "zx%d" % k, T.z64[:, k * C + A:(k + 1) * C], pl(T.x2, k, 1, B), scale=64.0)

        lists(0)
        far2(0, 0), far2(0, 1), self0(0), self0(1)
        high(3), add(2, 2), sub(2, 2)
        far2(0, 2), far2(0, 3), self0(2), self0(3)
        relist(1)
        self1(0), self1(1), self1(2), self1(3)
        for t in range(4):
            near2(0, t, 0), near2(0, t, 1)
        tt(keys("lo", range(4, 8)) + " " + keys("hi", range(4, 8)), keys("vv", range(4, 8)), T.vv[:, 0:4 * A], T.lo[:, 0:4 * A], T.hi[:, 0:4 * A], Op.add)
        tt(keys("vv", range(4, 8)) + " " + keys("xs", range(4)), "ft0", T.ft[:, 0:4 * A], T.vv[:, 0:4 * A], T.xs[:, 0:4 * A], Op.subtract)
        f0, l0 = 128 * r, (R - 1 - r) * A
        quant("ft ft0", "qf", T.qf[:, f0:f0 + 128], T.sf[:, f0:f0 + 128], T.ft[:])
        order("g", ["qf"], [])
        send(peer, T.ql[:, l0:l0 + A].bitcast(dt.uint8), T.qf[:, f0:f0 + A].bitcast(dt.uint8), T.sem["af%d" % r])
        send(peer, T.sl[:, l0:l0 + A], T.sf[:, f0:f0 + A], T.sem["af%d" % r])
        wrote["ql"] = [("af%d" % r, 2 * ne)]
        lists(1)
        far2(1, 0), far2(1, 1), far2(1, 2), far2(1, 3)
        ts("ft0", "f64", T.f64[:], T.ft[:, 0:4 * A], 64.0, None, Op.mult)
        if r == 0:
            quant("vb", "qv", T.qv[:], T.sv[:], T.vb[:])
        near2(1, 0, 0), near2(1, 0, 1), near2(1, 1, 0), near2(1, 1, 1), near2(1, 2, 0), add2(0)
        near2(1, 2, 1), sub2(0), near2(1, 3, 0), near2(1, 3, 1), add2(2), sub2(2)
        for b in range(4):
            mm("w ql qlz", "pw%d" % b, T["pw%d" % b][:, 0:128], pl(T.qw, b, 1, 128), pl(T.sw, b, 1, 128),
               T.ql[:, l0:l0 + 128], T.sl[:, l0:l0 + 128])
        for b in range(4):
            tt("pw%d f64" % b, "zh%d" % b, T.z64[:, b * C:b * C + A], T["pw%d" % b][:, 0:A], T.f64[:, b:4 * A:4], Op.add)
        for t in range(4):
            src = pl(T.z64, t).indirect(T.ru[:, 0:M])
            if t < 2:
                act("zx%d zh%d ru" % (t, t), "xn%d" % t, T.xn[:, t:4 * C:4], src, scale=0.015625)
            else:
                ts("zx%d zh%d ru" % (t, t), "xn%d" % t, T.xn[:, t:4 * C:4], src, 0.015625, None, Op.mult)
        quant(XN, "qx", T.qx[:], T.sx[:], T.xn[:])

    mm("qv qx", "pa", T.pa[:, 0:C], T.qv[:], T.sv[:], T.qx[:], T.sx[:])
    order("y", ["qx"], [])
    g.sync.dma_start(T.oc[:], T.qx[:].bitcast(dt.uint8)).then_inc(T.sem.st, 16)
    order("s", ["qx"], [])
    for k in range(4):
        (g.scalar, g.sync)[k % 2].dma_start(T.osc[4 * k:4 * k + 4, :], T.sx[32 * k:32 * k + 4, :]).then_inc(T.sem.st, 16)
    cp("pa", "ys", T.ys[:], T.pa[:, 0:C])
    order("s", ["ys"], [])
    g.scalar.dma_start(T.y[:], T.ys[:]).then_inc(T.sem.st, 16)
    need("g", [("ev", count["v"]), ("es", count["s"]), ("et", count["t"]), ("eg", count["g"]),
               ("sent", writes[0]), ("st", 96)])
